import numpy as np
import ml_dtypes


def mxq(x, axis, fmt="e4m3"):
    dtype, down = {"e4m3": (ml_dtypes.float8_e4m3fn, 7), "e5m2": (ml_dtypes.float8_e5m2, 14)}[fmt]
    v = np.moveaxis(np.asarray(x, np.float32).astype(ml_dtypes.bfloat16).astype(np.float64), axis, -1)
    blocks = v.reshape(v.shape[:-1] + (-1, 32))
    amax = np.abs(blocks).max(-1, keepdims=True)
    byte = np.maximum(np.where(amax > 0, np.frexp(amax)[1] - 1 + 127, 0) - down, 1)
    scale = np.exp2(byte - 127.0)
    codes = (blocks / scale).astype(np.float32).astype(dtype).astype(np.float64)
    return np.moveaxis((codes * scale).reshape(v.shape), -1, axis)


WIDE = False


def mx_kscale(k):
    if not WIDE:
        return np.ones(k)
    levels = np.array([10, -10, 5, -5, 0])
    if k % 512:
        return np.exp2(np.random.permutation(np.resize(levels, k // 32))).repeat(32)
    a = np.empty((k // 512, 16))
    for p in range(k // 512):
        a[p, :8] = np.random.permutation(np.resize(levels, 8))
        for g in range(8):
            far = levels[np.abs(levels - a[p, g]) >= 10]
            a[p, g + 8] = far[np.random.randint(len(far))]
    return np.exp2(a.ravel()).repeat(32)


def f64(x):
    return np.asarray(x).astype(np.float64)


def striped(idx):
    return np.tile(idx.reshape(-1, 16).T, (8, 1)).astype(np.uint16)


def unstriped(offs):
    return offs[:16].T.reshape(-1).astype(np.int64)


def pack_weight(w):
    k, n = w.shape
    w = f64(np.asarray(w, np.float32).astype(ml_dtypes.bfloat16)).reshape(k // 32, 32, n)
    amax = np.abs(w).max(1)
    byte = np.clip(np.where(amax > 0, np.frexp(amax)[1] - 1 + 127 - 7, 1), 1, 254)
    scaled = (w * np.exp2(127.0 - byte)[:, None, :]).reshape(k, n).astype(np.float32)
    words = np.ascontiguousarray(scaled.reshape(k // 512, 128, 4, n).transpose(0, 1, 3, 2)).astype(ml_dtypes.float8_e4m3fn).view(np.uint8)
    return words, np.ascontiguousarray(byte.astype(np.uint8).reshape(k // 512, 16, n))


def unpack_weight(words, scales):
    g, p, n, _ = words.shape
    vals = np.ascontiguousarray(words).view(ml_dtypes.float8_e4m3fn).astype(np.float64) * np.repeat(np.exp2(scales.astype(np.float64) - 127.0), 8, axis=1)[..., None]
    return vals.transpose(0, 1, 3, 2).reshape(g * 512, n)


def planes(y):
    n, m = y.shape
    v = y.astype(np.float32).astype(ml_dtypes.bfloat16).astype(np.float64).reshape(n // 32, 32, m)
    top = np.abs(v).max(1)
    byte = np.clip(np.where(top > 0, np.frexp(top)[1] - 1 + 127 - 7, 1), 1, 254)
    codes = (v * np.exp2(127.0 - byte)[:, None, :]).reshape(n, m).astype(np.float32).astype(ml_dtypes.float8_e4m3fn).view(np.uint8)
    words = codes.reshape(n // 512, 128, 4, m).transpose(0, 1, 3, 2)
    return np.ascontiguousarray(words), np.ascontiguousarray(byte.astype(np.uint8).reshape(n // 512, 16, m))


def relu(v):
    return np.maximum(v, 0.0)


K, T, S, J = 512, 2048, 512, 512


def setup_inputs():
    n = np.random.standard_normal
    s = mx_kscale(K)[:, None]
    packed_xT = pack_weight(n((K, T)) * s)
    return {
        "x_words": packed_xT[0],
        "x_scales": packed_xT[1],
        "hT": (n((K, J)) / np.sqrt(K) / s).astype(np.float32),
        "label": (np.random.uniform(0.0, 1.0, (S, J))).astype(np.float32),
        "offs": striped(np.random.permutation(T)[:S]),
    }


def reference(x_words, x_scales, hT, label, offs):
    xq = unpack_weight(x_words, x_scales)[:, unstriped(offs)]
    hTq = mxq(f64(hT), 0, "e4m3")
    y = xq.T @ hTq
    out_0 = relu(y + f64(label))
    return (out_0,) + planes(out_0)

@@ -1,0 +1,119 @@
+from contextlib import ExitStack
+
+import concourse.mybir as mybir
+
+K, T, S, J = 512, 2048, 512, 512
+FLOPS = 2 * K * S * J
+
+F32 = mybir.dt.float32
+BF16 = mybir.dt.bfloat16
+I32 = mybir.dt.int32
+U32 = mybir.dt.uint32
+U16 = mybir.dt.uint16
+U8 = mybir.dt.uint8
+FP8X4 = mybir.dt.float8_e4m3fn_x4
+ALU = mybir.AluOpType
+
+P = 128
+PACK = 4
+HALF = J // 2
+STEP = 128
+
+
+def tile_picked_znceg_hinge_po_kernel(tc, x_words, x_scales, hT, label, offs, out_0, out_1, out_2):
+    nc = tc.nc
+    h_rows = hT.rearrange("(p t) j -> p t j", t=PACK)
+    label_rows = label.rearrange("(p t) j -> p t j", t=PACK)
+    out_rows = out_0.rearrange("(p t) j -> p t j", t=PACK)
+    x_words_i32 = x_words[0].rearrange("p c t -> p (c t)").bitcast(I32)
+    x_scales_i32 = x_scales[0].bitcast(I32).rearrange("(q r) c -> r q c", r=PACK)
+    out_words_i32 = out_1[0].rearrange("p c t -> p (c t)").bitcast(I32)
+    out_scales_i32 = out_2[0].bitcast(I32).rearrange("(q r) c -> r q c", r=PACK)
+
+    with ExitStack() as ctx:
+        sb = ctx.enter_context(tc.tile_pool(name="sb", bufs=1))
+        psum = ctx.enter_context(tc.psum_pool(name="psum", bufs=1))
+
+        offsets = sb.tile([P, S // 16], U16, name="offsets")
+        word_table = sb.tile([P, T], I32, name="word_table", align_bytes=64)
+        scale_table = sb.tile([P, T], U8, name="scale_table", align_bytes=64)
+        h_raw = [sb.tile([P, PACK, HALF], F32, name=f"h_raw{i}", align_bytes=64) for i in range(2)]
+        label_sb = [sb.tile([P, PACK, HALF], F32, name=f"label{i}", align_bytes=64) for i in range(2)]
+
+        nc.gpsimd.memset(scale_table[:].bitcast(I32), 0)
+        nc.sync.dma_start(offsets[:], offs)
+        nc.sync.dma_start(h_raw[0][:], h_rows[:, :, 0:HALF])
+        for r in range(PACK):
+            nc.sync.dma_start(scale_table[r:P:32, :].bitcast(I32), x_scales_i32[r])
+        nc.sync.dma_start(word_table[:], x_words_i32)
+        nc.sync.dma_start(label_sb[0][:], label_rows[:, :, 0:HALF])
+        nc.sync.dma_start(h_raw[1][:], h_rows[:, :, HALF:J])
+        nc.sync.dma_start(label_sb[1][:], label_rows[:, :, HALF:J])
+
+        steps = J // STEP
+        h_codes, h_scales = [], []
+
+        def quantise_h(q):
+            half, c0 = divmod(q * STEP, HALF)
+            h_bf = sb.tile([P, STEP, PACK], BF16, name=f"h_bf{q}", align_bytes=64)
+            nc.scalar.copy(
+                h_bf[:].rearrange("p (c i) t -> p c t i", i=4),
+                h_raw[half][:, :, c0 : c0 + STEP].rearrange("p t (c i) -> p c t i", i=4),
+            )
+            codes = sb.tile([P, STEP], U32, name=f"h_codes{q}", align_bytes=64)
+            scales = sb.tile([P, STEP], U8, name=f"h_scales{q}", align_bytes=64)
+            nc.vector.quantize_mx(out=codes[:].bitcast(FP8X4), scales=scales[:], in_=h_bf[:].rearrange("p c t -> p (c t)"))
+            h_codes.append(codes)
+            h_scales.append(scales)
+
+        picked_scales = sb.tile([P, S], U8, name="picked_scales", align_bytes=64)
+        dealt_scales = sb.tile([P, PACK, P], U8, name="dealt_scales", align_bytes=64)
+        picked_words = sb.tile([P, S], U32, name="picked_words", align_bytes=64)
+        dealt_words = sb.tile([P, PACK, P], U32, name="dealt_words", align_bytes=64)
+        nc.vector.tensor_copy(picked_scales[:], scale_table[:].indirect(offsets[:]))
+        quantise_h(0)
+        nc.vector.tensor_copy(
+            dealt_scales[:].rearrange("p t m -> p m t"), picked_scales[:].rearrange("p (m t) -> p m t", t=PACK)
+        )
+        quantise_h(1)
+        nc.vector.tensor_copy(picked_words[:], word_table[:].bitcast(U32).indirect(offsets[:]))
+        nc.vector.tensor_copy(
+            dealt_words[:].rearrange("p t m -> p m t"), picked_words[:].rearrange("p (m t) -> p m t", t=PACK)
+        )
+        quantise_h(2)
+        quantise_h(3)
+
+        out_codes = [sb.tile([P, HALF], I32, name=f"out_codes{i}", align_bytes=64) for i in range(2)]
+        out_scales = sb.tile([P, J], U8, name="out_scales", align_bytes=64)
+        for q in range(steps):
+            half, c0 = divmod(q * STEP, HALF)
+            acc = psum.tile([P, PACK, STEP], F32, name=f"acc{q}")
+            for t in range(PACK):
+                nc.tensor.matmul_mx(
+                    out=acc[:, t, :],
+                    lhsT=dealt_words[:, t, :].bitcast(FP8X4),
+                    lhsT_scale=dealt_scales[:, t, :],
+                    rhs=h_codes[q][:].bitcast(FP8X4),
+                    rhs_scale=h_scales[q][:],
+                    start=True,
+                    stop=True,
+                )
+            margin = sb.tile([P, PACK, STEP], F32, name=f"margin{q}", align_bytes=64)
+            nc.vector.tensor_tensor(margin[:], acc[:], label_sb[half][:, :, c0 : c0 + STEP], ALU.add)
+            hinge = sb.tile([P, PACK, STEP], F32, name=f"hinge{q}", align_bytes=64)
+            nc.vector.tensor_scalar_max(hinge[:], margin[:], 0.0)
+            nc.sync.dma_start(out_rows[:, :, q * STEP : (q + 1) * STEP], hinge[:])
+            hinge_bf = sb.tile([P, STEP, PACK], BF16, name=f"hinge_bf{q}", align_bytes=64)
+            nc.scalar.copy(
+                hinge_bf[:].rearrange("p (c i) t -> p c t i", i=4),
+                hinge[:].rearrange("p t (c i) -> p c t i", i=4),
+            )
+            nc.vector.quantize_mx(
+                out=out_codes[half][:, c0 : c0 + STEP].bitcast(FP8X4),
+                scales=out_scales[:, q * STEP : (q + 1) * STEP],
+                in_=hinge_bf[:].rearrange("p c t -> p (c t)"),
+            )
+            if c0 + STEP == HALF:
+                nc.sync.dma_start(out_words_i32[:, half * HALF : (half + 1) * HALF], out_codes[half][:])
+        for r in range(PACK):
+            nc.sync.dma_start(out_scales_i32[r], out_scales[r:P:32, :].bitcast(I32))

@@ -13,11 +13,30 @@ U16 = mybir.dt.uint16
 U8 = mybir.dt.uint8
 FP8X4 = mybir.dt.float8_e4m3fn_x4
 ALU = mybir.AluOpType
+RELU = mybir.ActivationFunctionType.Relu
 
 P = 128
 PACK = 4
-HALF = J // 2
-STEP = 128
+WIDTHS = [128,128,128,128]
+H_LOADS = [128,128,128,128]
+L_LOADS = [128,128,128,128]
+W_STORES = [256,256]
+
+
+def spans(widths):
+    starts = [sum(widths[:i]) for i in range(len(widths))]
+    return [(a, a + w) for a, w in zip(starts, widths)]
+
+
+def locate(parts, c0):
+    for i, (a, b) in enumerate(parts):
+        if a <= c0 < b:
+            return i, c0 - a
+    raise ValueError(c0)
+
+
+def by_line(ap, text):
+    return ap.rearrange(text, i=4)
 
 
 def tile_picked_znceg_hinge_po_kernel(tc, x_words, x_scales, hT, label, offs, out_0, out_1, out_2):
@@ -29,6 +48,7 @@ def tile_picked_znceg_hinge_po_kernel(tc, x_words, x_scales, hT, label, offs, ou
     x_scales_i32 = x_scales[0].bitcast(I32).rearrange("(q r) c -> r q c", r=PACK)
     out_words_i32 = out_1[0].rearrange("p c t -> p (c t)").bitcast(I32)
     out_scales_i32 = out_2[0].bitcast(I32).rearrange("(q r) c -> r q c", r=PACK)
+    steps, h_parts, l_parts, w_parts = spans(WIDTHS), spans(H_LOADS), spans(L_LOADS), spans(W_STORES)
 
     with ExitStack() as ctx:
         sb = ctx.enter_context(tc.tile_pool(name="sb", bufs=1))
@@ -37,83 +57,118 @@ def tile_picked_znceg_hinge_po_kernel(tc, x_words, x_scales, hT, label, offs, ou
         offsets = sb.tile([P, S // 16], U16, name="offsets")
         word_table = sb.tile([P, T], I32, name="word_table", align_bytes=64)
         scale_table = sb.tile([P, T], U8, name="scale_table", align_bytes=64)
-        h_raw = [sb.tile([P, PACK, HALF], F32, name=f"h_raw{i}", align_bytes=64) for i in range(2)]
-        label_sb = [sb.tile([P, PACK, HALF], F32, name=f"label{i}", align_bytes=64) for i in range(2)]
+        h_raw = [sb.tile([P, PACK, b - a], F32, name=f"h_raw{i}", align_bytes=64) for i, (a, b) in enumerate(h_parts)]
+        label_sb = [sb.tile([P, PACK, b - a], F32, name=f"label{i}", align_bytes=64) for i, (a, b) in enumerate(l_parts)]
 
-        nc.gpsimd.memset(scale_table[:].bitcast(I32), 0)
+        def load_h(i):
+            nc.sync.dma_start(h_raw[i][:], h_rows[:, :, h_parts[i][0] : h_parts[i][1]])
+
+        def load_l(i):
+            nc.sync.dma_start(label_sb[i][:], label_rows[:, :, l_parts[i][0] : l_parts[i][1]])
+
+        nc.vector.memset(scale_table[:, : T // 2].bitcast(I32), 0)
+        nc.gpsimd.memset(scale_table[:, T // 2 :].bitcast(I32), 0)
         nc.sync.dma_start(offsets[:], offs)
-        nc.sync.dma_start(h_raw[0][:], h_rows[:, :, 0:HALF])
+        nc.sync.dma_start(word_table[:, 0:256], x_words_i32[:, 0:256])
+        nc.sync.dma_start(word_table[:, 256:512], x_words_i32[:, 256:512])
         for r in range(PACK):
             nc.sync.dma_start(scale_table[r:P:32, :].bitcast(I32), x_scales_i32[r])
-        nc.sync.dma_start(word_table[:], x_words_i32)
-        nc.sync.dma_start(label_sb[0][:], label_rows[:, :, 0:HALF])
-        nc.sync.dma_start(h_raw[1][:], h_rows[:, :, HALF:J])
-        nc.sync.dma_start(label_sb[1][:], label_rows[:, :, HALF:J])
-
-        steps = J // STEP
-        h_codes, h_scales = [], []
-
-        def quantise_h(q):
-            half, c0 = divmod(q * STEP, HALF)
-            h_bf = sb.tile([P, STEP, PACK], BF16, name=f"h_bf{q}", align_bytes=64)
-            nc.scalar.copy(
-                h_bf[:].rearrange("p (c i) t -> p c t i", i=4),
-                h_raw[half][:, :, c0 : c0 + STEP].rearrange("p t (c i) -> p c t i", i=4),
-            )
-            codes = sb.tile([P, STEP], U32, name=f"h_codes{q}", align_bytes=64)
-            scales = sb.tile([P, STEP], U8, name=f"h_scales{q}", align_bytes=64)
-            nc.vector.quantize_mx(out=codes[:].bitcast(FP8X4), scales=scales[:], in_=h_bf[:].rearrange("p c t -> p (c t)"))
-            h_codes.append(codes)
-            h_scales.append(scales)
+        nc.sync.dma_start(word_table[:, 512:2048], x_words_i32[:, 512:2048])
+        load_h(0)
+        load_h(1)
+        load_l(0)
+        load_h(2)
+        load_l(1)
+        load_h(3)
+        load_l(2)
+        load_l(3)
 
         picked_scales = sb.tile([P, S], U8, name="picked_scales", align_bytes=64)
         dealt_scales = sb.tile([P, PACK, P], U8, name="dealt_scales", align_bytes=64)
-        picked_words = sb.tile([P, S], U32, name="picked_words", align_bytes=64)
         dealt_words = sb.tile([P, PACK, P], U32, name="dealt_words", align_bytes=64)
         nc.vector.tensor_copy(picked_scales[:], scale_table[:].indirect(offsets[:]))
-        quantise_h(0)
         nc.vector.tensor_copy(
             dealt_scales[:].rearrange("p t m -> p m t"), picked_scales[:].rearrange("p (m t) -> p m t", t=PACK)
         )
-        quantise_h(1)
-        nc.vector.tensor_copy(picked_words[:], word_table[:].bitcast(U32).indirect(offsets[:]))
-        nc.vector.tensor_copy(
-            dealt_words[:].rearrange("p t m -> p m t"), picked_words[:].rearrange("p (m t) -> p m t", t=PACK)
-        )
-        quantise_h(2)
-        quantise_h(3)
+        nc.vector.tensor_copy(dealt_words[:].rearrange("p t m -> p m t"), word_table[:].bitcast(U32).indirect(offsets[:]))
 
-        out_codes = [sb.tile([P, HALF], I32, name=f"out_codes{i}", align_bytes=64) for i in range(2)]
+        out_codes = [sb.tile([P, b - a], I32, name=f"out_codes{i}", align_bytes=64) for i, (a, b) in enumerate(w_parts)]
         out_scales = sb.tile([P, J], U8, name="out_scales", align_bytes=64)
-        for q in range(steps):
-            half, c0 = divmod(q * STEP, HALF)
-            acc = psum.tile([P, PACK, STEP], F32, name=f"acc{q}")
+        h_bf, acc, margin, hinge_bf = {}, {}, {}, {}
+
+        def cast_h(q):
+            a, b = steps[q]
+            i, c0 = locate(h_parts, a)
+            h_bf[q] = sb.tile([P, b - a, PACK], BF16, name=f"h_bf{q}", align_bytes=64)
+            nc.scalar.copy(by_line(h_bf[q][:], "p (c i) t -> p c t i"), by_line(h_raw[i][:, :, c0 : c0 + b - a], "p t (c i) -> p c t i"))
+
+        def product(q):
+            a, b = steps[q]
+            codes = sb.tile([P, b - a], U32, name=f"h_codes{q}", align_bytes=64)
+            scales = sb.tile([P, b - a], U8, name=f"h_scales{q}", align_bytes=64)
+            nc.vector.quantize_mx(out=codes[:].bitcast(FP8X4), scales=scales[:], in_=h_bf[q][:].rearrange("p c t -> p (c t)"))
+            acc[q] = psum.tile([P, PACK, b - a], F32, name=f"acc{q}")
             for t in range(PACK):
                 nc.tensor.matmul_mx(
-                    out=acc[:, t, :],
+                    out=acc[q][:, t, :],
                     lhsT=dealt_words[:, t, :].bitcast(FP8X4),
                     lhsT_scale=dealt_scales[:, t, :],
-                    rhs=h_codes[q][:].bitcast(FP8X4),
-                    rhs_scale=h_scales[q][:],
+                    rhs=codes[:].bitcast(FP8X4),
+                    rhs_scale=scales[:],
                     start=True,
                     stop=True,
                 )
-            margin = sb.tile([P, PACK, STEP], F32, name=f"margin{q}", align_bytes=64)
-            nc.vector.tensor_tensor(margin[:], acc[:], label_sb[half][:, :, c0 : c0 + STEP], ALU.add)
-            hinge = sb.tile([P, PACK, STEP], F32, name=f"hinge{q}", align_bytes=64)
-            nc.vector.tensor_scalar_max(hinge[:], margin[:], 0.0)
-            nc.sync.dma_start(out_rows[:, :, q * STEP : (q + 1) * STEP], hinge[:])
-            hinge_bf = sb.tile([P, STEP, PACK], BF16, name=f"hinge_bf{q}", align_bytes=64)
-            nc.scalar.copy(
-                hinge_bf[:].rearrange("p (c i) t -> p c t i", i=4),
-                hinge[:].rearrange("p t (c i) -> p c t i", i=4),
-            )
+
+        def add_label(q):
+            a, b = steps[q]
+            i, c0 = locate(l_parts, a)
+            margin[q] = sb.tile([P, PACK, b - a], F32, name=f"margin{q}", align_bytes=64)
+            nc.vector.tensor_tensor(margin[q][:], acc[q][:], label_sb[i][:, :, c0 : c0 + b - a], ALU.add)
+            hinge = sb.tile([P, PACK, b - a], F32, name=f"hinge{q}", align_bytes=64)
+            nc.scalar.activation(hinge[:], margin[q][:], RELU)
+            nc.sync.dma_start(out_rows[:, :, a:b], hinge[:])
+
+        def round_out(q):
+            a, b = steps[q]
+            hinge_bf[q] = sb.tile([P, b - a, PACK], BF16, name=f"hinge_bf{q}", align_bytes=64)
+            nc.vector.tensor_scalar_max(by_line(hinge_bf[q][:], "p (c i) t -> p c t i"), by_line(margin[q][:], "p t (c i) -> p c t i"), 0.0)
+
+        def round_out_scalar(q):
+            a, b = steps[q]
+            hinge_bf[q] = sb.tile([P, b - a, PACK], BF16, name=f"hinge_bf{q}", align_bytes=64)
+            nc.scalar.activation(by_line(hinge_bf[q][:], "p (c i) t -> p c t i"), by_line(margin[q][:], "p t (c i) -> p c t i"), RELU)
+
+        def quantise_out(q):
+            a, b = steps[q]
+            i, c0 = locate(w_parts, a)
             nc.vector.quantize_mx(
-                out=out_codes[half][:, c0 : c0 + STEP].bitcast(FP8X4),
-                scales=out_scales[:, q * STEP : (q + 1) * STEP],
-                in_=hinge_bf[:].rearrange("p c t -> p (c t)"),
+                out=out_codes[i][:, c0 : c0 + b - a].bitcast(FP8X4),
+                scales=out_scales[:, a:b],
+                in_=hinge_bf[q][:].rearrange("p c t -> p (c t)"),
             )
-            if c0 + STEP == HALF:
-                nc.sync.dma_start(out_words_i32[:, half * HALF : (half + 1) * HALF], out_codes[half][:])
+            if b == w_parts[i][1]:
+                nc.sync.dma_start(out_words_i32[:, w_parts[i][0] : b], out_codes[i][:])
+
+        cast_h(0)
+        cast_h(1)
+        product(0)
+        product(1)
+        add_label(0)
+        cast_h(2)
+        round_out_scalar(0)
+        product(2)
+        add_label(1)
+        cast_h(3)
+        quantise_out(0)
+        product(3)
+        round_out(1)
+        add_label(2)
+        quantise_out(1)
+        round_out(2)
+        add_label(3)
+        quantise_out(2)
+        round_out(3)
+        quantise_out(3)
         for r in range(PACK):
-            nc.sync.dma_start(out_scales_i32[r], out_scales[r:P:32, :].bitcast(I32))
+            queue = nc.scalar if r % 2 == 0 else nc.sync
+            queue.dma_start(out_scales_i32[r], out_scales[r:P:32, :].bitcast(I32))

@@ -17,22 +17,8 @@ RELU = mybir.ActivationFunctionType.Relu
 
 P = 128
 PACK = 4
-WIDTHS = [128,128,128,128]
-H_LOADS = [128,128,128,128]
-L_LOADS = [128,128,128,128]
-W_STORES = [256,256]
-
-
-def spans(widths):
-    starts = [sum(widths[:i]) for i in range(len(widths))]
-    return [(a, a + w) for a, w in zip(starts, widths)]
-
-
-def locate(parts, c0):
-    for i, (a, b) in enumerate(parts):
-        if a <= c0 < b:
-            return i, c0 - a
-    raise ValueError(c0)
+HALF = J // 2
+QUARTER = J // 4
 
 
 def by_line(ap, text):
@@ -48,23 +34,23 @@ def tile_picked_znceg_hinge_po_kernel(tc, x_words, x_scales, hT, label, offs, ou
     x_scales_i32 = x_scales[0].bitcast(I32).rearrange("(q r) c -> r q c", r=PACK)
     out_words_i32 = out_1[0].rearrange("p c t -> p (c t)").bitcast(I32)
     out_scales_i32 = out_2[0].bitcast(I32).rearrange("(q r) c -> r q c", r=PACK)
-    steps, h_parts, l_parts, w_parts = spans(WIDTHS), spans(H_LOADS), spans(L_LOADS), spans(W_STORES)
 
     with ExitStack() as ctx:
         sb = ctx.enter_context(tc.tile_pool(name="sb", bufs=1))
+        ring = ctx.enter_context(tc.tile_pool(name="ring", bufs=3))
         psum = ctx.enter_context(tc.psum_pool(name="psum", bufs=1))
 
         offsets = sb.tile([P, S // 16], U16, name="offsets")
         word_table = sb.tile([P, T], I32, name="word_table", align_bytes=64)
         scale_table = sb.tile([P, T], U8, name="scale_table", align_bytes=64)
-        h_raw = [sb.tile([P, PACK, b - a], F32, name=f"h_raw{i}", align_bytes=64) for i, (a, b) in enumerate(h_parts)]
-        label_sb = [sb.tile([P, PACK, b - a], F32, name=f"label{i}", align_bytes=64) for i, (a, b) in enumerate(l_parts)]
+        h_raw = [sb.tile([P, PACK, HALF], F32, name=f"h_raw{i}", align_bytes=64) for i in range(2)]
+        label_sb = [sb.tile([P, 2, J], F32, name=f"label{i}", align_bytes=64) for i in range(2)]
 
         def load_h(i):
-            nc.sync.dma_start(h_raw[i][:], h_rows[:, :, h_parts[i][0] : h_parts[i][1]])
+            nc.sync.dma_start(h_raw[i][:], h_rows[:, :, i * HALF : (i + 1) * HALF])
 
-        def load_l(i):
-            nc.sync.dma_start(label_sb[i][:], label_rows[:, :, l_parts[i][0] : l_parts[i][1]])
+        def load_label(i):
+            nc.sync.dma_start(label_sb[i][:], label_rows[:, 2 * i : 2 * i + 2, :])
 
         nc.vector.memset(scale_table[:, : T // 2].bitcast(I32), 0)
         nc.gpsimd.memset(scale_table[:, T // 2 :].bitcast(I32), 0)
@@ -73,15 +59,11 @@ def tile_picked_znceg_hinge_po_kernel(tc, x_words, x_scales, hT, label, offs, ou
         nc.sync.dma_start(word_table[:, 256:512], x_words_i32[:, 256:512])
         for r in range(PACK):
             nc.sync.dma_start(scale_table[r:P:32, :].bitcast(I32), x_scales_i32[r])
-        nc.sync.dma_start(word_table[:, 512:2048], x_words_i32[:, 512:2048])
+        nc.sync.dma_start(word_table[:, 512:T], x_words_i32[:, 512:T])
         load_h(0)
         load_h(1)
-        load_l(0)
-        load_h(2)
-        load_l(1)
-        load_h(3)
-        load_l(2)
-        load_l(3)
+        load_label(0)
+        load_label(1)
 
         picked_scales = sb.tile([P, S], U8, name="picked_scales", align_bytes=64)
         dealt_scales = sb.tile([P, PACK, P], U8, name="dealt_scales", align_bytes=64)
@@ -92,25 +74,36 @@ def tile_picked_znceg_hinge_po_kernel(tc, x_words, x_scales, hT, label, offs, ou
         )
         nc.vector.tensor_copy(dealt_words[:].rearrange("p t m -> p m t"), word_table[:].bitcast(U32).indirect(offsets[:]))
 
-        out_codes = [sb.tile([P, b - a], I32, name=f"out_codes{i}", align_bytes=64) for i, (a, b) in enumerate(w_parts)]
+        h_bf = {}
+        margin = [sb.tile([P, PACK, HALF], F32, name=f"margin{v}", align_bytes=64) for v in range(2)]
+        hinge_bf = [sb.tile([P, HALF, PACK], BF16, name=f"hinge_bf{v}", align_bytes=64) for v in range(2)]
+        hinge_sb = [[sb.tile([P, 2, HALF], F32, name=f"hinge{u}{v}", align_bytes=64) for v in range(2)] for u in range(2)]
+        out_codes = sb.tile([P, J], I32, name="out_codes", align_bytes=64)
         out_scales = sb.tile([P, J], U8, name="out_scales", align_bytes=64)
-        h_bf, acc, margin, hinge_bf = {}, {}, {}, {}
+        acc = [[psum.tile([P, 2, HALF], F32, name=f"acc{u}{v}") for v in range(2)] for u in range(2)]
 
-        def cast_h(q):
-            a, b = steps[q]
-            i, c0 = locate(h_parts, a)
-            h_bf[q] = sb.tile([P, b - a, PACK], BF16, name=f"h_bf{q}", align_bytes=64)
-            nc.scalar.copy(by_line(h_bf[q][:], "p (c i) t -> p c t i"), by_line(h_raw[i][:, :, c0 : c0 + b - a], "p t (c i) -> p c t i"))
+        def cast_h(q, on_vector):
+            v, c0 = divmod(q * QUARTER, HALF)
+            h_bf[q] = ring.tile([P, QUARTER, PACK], BF16, name="h_bf", align_bytes=64)
+            dst = by_line(h_bf[q][:], "p (c i) t -> p c t i")
+            src = by_line(h_raw[v][:, :, c0 : c0 + QUARTER], "p t (c i) -> p c t i")
+            if on_vector:
+                nc.vector.tensor_copy(dst, src)
+            else:
+                nc.scalar.copy(dst, src)
 
         def product(q):
-            a, b = steps[q]
-            codes = sb.tile([P, b - a], U32, name=f"h_codes{q}", align_bytes=64)
-            scales = sb.tile([P, b - a], U8, name=f"h_scales{q}", align_bytes=64)
-            nc.vector.quantize_mx(out=codes[:].bitcast(FP8X4), scales=scales[:], in_=h_bf[q][:].rearrange("p c t -> p (c t)"))
-            acc[q] = psum.tile([P, PACK, b - a], F32, name=f"acc{q}")
+            v, c0 = divmod(q * QUARTER, HALF)
+            codes = sb.tile([P, QUARTER], U32, name=f"h_codes{q}", align_bytes=64)
+            scales = sb.tile([P, QUARTER], U8, name=f"h_scales{q}", align_bytes=64)
+            nc.vector.quantize_mx(
+                out=codes[:].bitcast(FP8X4),
+                scales=scales[:],
+                in_=h_bf[q][:].rearrange("p c t -> p (c t)"),
+            )
             for t in range(PACK):
                 nc.tensor.matmul_mx(
-                    out=acc[q][:, t, :],
+                    out=acc[t // 2][v][:, t % 2, c0 : c0 + QUARTER],
                     lhsT=dealt_words[:, t, :].bitcast(FP8X4),
                     lhsT_scale=dealt_scales[:, t, :],
                     rhs=codes[:].bitcast(FP8X4),
@@ -119,56 +112,67 @@ def tile_picked_znceg_hinge_po_kernel(tc, x_words, x_scales, hT, label, offs, ou
                     stop=True,
                 )
 
-        def add_label(q):
-            a, b = steps[q]
-            i, c0 = locate(l_parts, a)
-            margin[q] = sb.tile([P, PACK, b - a], F32, name=f"margin{q}", align_bytes=64)
-            nc.vector.tensor_tensor(margin[q][:], acc[q][:], label_sb[i][:, :, c0 : c0 + b - a], ALU.add)
-            hinge = sb.tile([P, PACK, b - a], F32, name=f"hinge{q}", align_bytes=64)
-            nc.scalar.activation(hinge[:], margin[q][:], RELU)
-            nc.sync.dma_start(out_rows[:, :, a:b], hinge[:])
+        def add_label(u, v):
+            part = label_sb[u][:, :, v * HALF : (v + 1) * HALF]
+            nc.vector.tensor_tensor(margin[v][:, 2 * u : 2 * u + 2, :], acc[u][v][:], part, ALU.add)
 
-        def round_out(q):
-            a, b = steps[q]
-            hinge_bf[q] = sb.tile([P, b - a, PACK], BF16, name=f"hinge_bf{q}", align_bytes=64)
-            nc.vector.tensor_scalar_max(by_line(hinge_bf[q][:], "p (c i) t -> p c t i"), by_line(margin[q][:], "p t (c i) -> p c t i"), 0.0)
+        def hinge(u, v, engine, store):
+            dst = hinge_sb[u][v][:]
+            src = margin[v][:, 2 * u : 2 * u + 2, :]
+            if engine == "s":
+                nc.scalar.activation(dst, src, RELU)
+            elif engine == "v":
+                nc.vector.tensor_scalar_max(dst, src, 0.0)
+            else:
+                nc.gpsimd.tensor_scalar(dst, src, 3.0e38, 0.0, ALU.min, ALU.max)
+            if store:
+                nc.sync.dma_start(out_rows[:, 2 * u : 2 * u + 2, v * HALF : (v + 1) * HALF], dst)
 
-        def round_out_scalar(q):
-            a, b = steps[q]
-            hinge_bf[q] = sb.tile([P, b - a, PACK], BF16, name=f"hinge_bf{q}", align_bytes=64)
-            nc.scalar.activation(by_line(hinge_bf[q][:], "p (c i) t -> p c t i"), by_line(margin[q][:], "p t (c i) -> p c t i"), RELU)
+        def store_pair(u):
+            nc.sync.dma_start(out_rows[:, 2 * u : 2 * u + 2, :], hinge_sb[u][:])
 
-        def quantise_out(q):
-            a, b = steps[q]
-            i, c0 = locate(w_parts, a)
+        def round_out(q, on_vector):
+            v, c0 = divmod(q * QUARTER, HALF)
+            dst = by_line(hinge_bf[v][:, c0 : c0 + QUARTER, :], "p (c i) t -> p c t i")
+            src = by_line(margin[v][:, :, c0 : c0 + QUARTER], "p t (c i) -> p c t i")
+            if on_vector:
+                nc.vector.tensor_scalar_max(dst, src, 0.0)
+            else:
+                nc.scalar.activation(dst, src, RELU)
+
+        def quantise_out(q0, q1):
+            v, c0 = divmod(q0 * QUARTER, HALF)
+            a, b = q0 * QUARTER, q1 * QUARTER
             nc.vector.quantize_mx(
-                out=out_codes[i][:, c0 : c0 + b - a].bitcast(FP8X4),
+                out=out_codes[:, a:b].bitcast(FP8X4),
                 scales=out_scales[:, a:b],
-                in_=hinge_bf[q][:].rearrange("p c t -> p (c t)"),
+                in_=hinge_bf[v][:, c0 : c0 + b - a, :].rearrange("p c t -> p (c t)"),
             )
-            if b == w_parts[i][1]:
-                nc.sync.dma_start(out_words_i32[:, w_parts[i][0] : b], out_codes[i][:])
+            if b % HALF == 0:
+                nc.sync.dma_start(out_words_i32[:, b - HALF : b], out_codes[:, b - HALF : b])
 
-        cast_h(0)
-        cast_h(1)
+        cast_h(0, False)
         product(0)
+        cast_h(1, False)
         product(1)
-        add_label(0)
-        cast_h(2)
-        round_out_scalar(0)
-        product(2)
-        add_label(1)
-        cast_h(3)
-        quantise_out(0)
+        cast_h(2, False)
+        cast_h(3, True)
         product(3)
-        round_out(1)
-        add_label(2)
-        quantise_out(1)
-        round_out(2)
-        add_label(3)
-        quantise_out(2)
-        round_out(3)
-        quantise_out(3)
+        product(2)
+        add_label(0, 0)
+        hinge(0, 0, "g", True)
+        add_label(0, 1)
+        hinge(0, 1, "g", True)
+        add_label(1, 0)
+        round_out(0, False)
+        round_out(1, False)
+        hinge(1, 0, "g", True)
+        add_label(1, 1)
+        hinge(1, 1, "s", True)
+        round_out(2, True)
+        round_out(3, True)
+        quantise_out(0, 2)
+        quantise_out(2, 4)
         for r in range(PACK):
             queue = nc.scalar if r % 2 == 0 else nc.sync
             queue.dma_start(out_scales_i32[r], out_scales[r:P:32, :].bitcast(I32))

@@ -44,13 +44,11 @@ def tile_picked_znceg_hinge_po_kernel(tc, x_words, x_scales, hT, label, offs, ou
         word_table = sb.tile([P, T], I32, name="word_table", align_bytes=64)
         scale_table = sb.tile([P, T], U8, name="scale_table", align_bytes=64)
         h_raw = [sb.tile([P, PACK, HALF], F32, name=f"h_raw{i}", align_bytes=64) for i in range(2)]
-        label_sb = [sb.tile([P, 2, J], F32, name=f"label{i}", align_bytes=64) for i in range(2)]
+        label_first = sb.tile([P, 2, J], F32, name="label_first", align_bytes=64)
+        label_second = [sb.tile([P, 2, HALF], F32, name=f"label_second{v}", align_bytes=64) for v in range(2)]
 
         def load_h(i):
             nc.sync.dma_start(h_raw[i][:], h_rows[:, :, i * HALF : (i + 1) * HALF])
-
-        def load_label(i):
-            nc.sync.dma_start(label_sb[i][:], label_rows[:, 2 * i : 2 * i + 2, :])
 
         nc.vector.memset(scale_table[:, : T // 2].bitcast(I32), 0)
         nc.gpsimd.memset(scale_table[:, T // 2 :].bitcast(I32), 0)
@@ -62,8 +60,9 @@ def tile_picked_znceg_hinge_po_kernel(tc, x_words, x_scales, hT, label, offs, ou
         nc.sync.dma_start(word_table[:, 512:T], x_words_i32[:, 512:T])
         load_h(0)
         load_h(1)
-        load_label(0)
-        load_label(1)
+        nc.sync.dma_start(label_first[:], label_rows[:, 0:2, :])
+        for v in range(2):
+            nc.sync.dma_start(label_second[v][:], label_rows[:, 2:4, v * HALF : (v + 1) * HALF])
 
         picked_scales = sb.tile([P, S], U8, name="picked_scales", align_bytes=64)
         dealt_scales = sb.tile([P, PACK, P], U8, name="dealt_scales", align_bytes=64)
@@ -113,7 +112,7 @@ def tile_picked_znceg_hinge_po_kernel(tc, x_words, x_scales, hT, label, offs, ou
                 )
 
         def add_label(u, v):
-            part = label_sb[u][:, :, v * HALF : (v + 1) * HALF]
+            part = label_second[v][:] if u else label_first[:, :, v * HALF : (v + 1) * HALF]
             nc.vector.tensor_tensor(margin[v][:, 2 * u : 2 * u + 2, :], acc[u][v][:], part, ALU.add)
 
         def hinge(u, v, engine, store):
@@ -127,9 +126,6 @@ def tile_picked_znceg_hinge_po_kernel(tc, x_words, x_scales, hT, label, offs, ou
                 nc.gpsimd.tensor_scalar(dst, src, 3.0e38, 0.0, ALU.min, ALU.max)
             if store:
                 nc.sync.dma_start(out_rows[:, 2 * u : 2 * u + 2, v * HALF : (v + 1) * HALF], dst)
-
-        def store_pair(u):
-            nc.sync.dma_start(out_rows[:, 2 * u : 2 * u + 2, :], hinge_sb[u][:])
 
         def round_out(q, on_vector):
             v, c0 = divmod(q * QUARTER, HALF)
@@ -160,16 +156,16 @@ def tile_picked_znceg_hinge_po_kernel(tc, x_words, x_scales, hT, label, offs, ou
         product(3)
         product(2)
         add_label(0, 0)
-        hinge(0, 0, "g", True)
-        add_label(0, 1)
-        hinge(0, 1, "g", True)
+        hinge(0, 0, "s", True)
         add_label(1, 0)
+        hinge(1, 0, "g", True)
         round_out(0, False)
         round_out(1, False)
-        hinge(1, 0, "g", True)
+        add_label(0, 1)
+        hinge(0, 1, "g", True)
         add_label(1, 1)
-        hinge(1, 1, "s", True)
-        round_out(2, True)
+        round_out(2, False)
+        hinge(1, 1, "v", True)
         round_out(3, True)
         quantise_out(0, 2)
         quantise_out(2, 4)

@@ -50,11 +50,10 @@ def tile_picked_znceg_hinge_po_kernel(tc, x_words, x_scales, hT, label, offs, ou
         def load_h(i):
             nc.sync.dma_start(h_raw[i][:], h_rows[:, :, i * HALF : (i + 1) * HALF])
 
-        nc.vector.memset(scale_table[:, : T // 2].bitcast(I32), 0)
-        nc.gpsimd.memset(scale_table[:, T // 2 :].bitcast(I32), 0)
+        nc.vector.memset(scale_table[:, : T - 1536].bitcast(I32), 0)
+        nc.gpsimd.memset(scale_table[:, T - 1536 :].bitcast(I32), 0)
         nc.sync.dma_start(offsets[:], offs)
-        nc.sync.dma_start(word_table[:, 0:256], x_words_i32[:, 0:256])
-        nc.sync.dma_start(word_table[:, 256:512], x_words_i32[:, 256:512])
+        nc.sync.dma_start(word_table[:, 0:512], x_words_i32[:, 0:512])
         for r in range(PACK):
             nc.sync.dma_start(scale_table[r:P:32, :].bitcast(I32), x_scales_i32[r])
         nc.sync.dma_start(word_table[:, 512:T], x_words_i32[:, 512:T])
@@ -158,14 +157,14 @@ def tile_picked_znceg_hinge_po_kernel(tc, x_words, x_scales, hT, label, offs, ou
         add_label(0, 0)
         hinge(0, 0, "s", True)
         add_label(1, 0)
-        hinge(1, 0, "g", True)
+        hinge(1, 0, "s", True)
         round_out(0, False)
         round_out(1, False)
         add_label(0, 1)
         hinge(0, 1, "g", True)
         add_label(1, 1)
-        round_out(2, False)
         hinge(1, 1, "v", True)
+        round_out(2, True)
         round_out(3, True)
         quantise_out(0, 2)
         quantise_out(2, 4)

@@ -122,7 +122,8 @@ def tile_picked_znceg_hinge_po_kernel(tc, x_words, x_scales, hT, label, offs, ou
             elif engine == "v":
                 nc.vector.tensor_scalar_max(dst, src, 0.0)
             else:
-                nc.gpsimd.tensor_scalar(dst, src, 3.0e38, 0.0, ALU.min, ALU.max)
+                nc.scalar.activation(dst[:, 0, :], src[:, 0, :], RELU)
+                nc.gpsimd.tensor_scalar(dst[:, 1, :], src[:, 1, :], 3.0e38, 0.0, ALU.min, ALU.max)
             if store:
                 nc.sync.dma_start(out_rows[:, 2 * u : 2 * u + 2, v * HALF : (v + 1) * HALF], dst)
 
@@ -155,13 +156,13 @@ def tile_picked_znceg_hinge_po_kernel(tc, x_words, x_scales, hT, label, offs, ou
         product(3)
         product(2)
         add_label(0, 0)
-        hinge(0, 0, "s", True)
+        hinge(0, 0, "g", True)
         add_label(1, 0)
-        hinge(1, 0, "s", True)
+        hinge(1, 0, "g", True)
         round_out(0, False)
-        round_out(1, False)
         add_label(0, 1)
         hinge(0, 1, "g", True)
+        round_out(1, False)
         add_label(1, 1)
         hinge(1, 1, "v", True)
         round_out(2, True)

@@ -17,12 +17,24 @@ RELU = mybir.ActivationFunctionType.Relu
 
 P = 128
 PACK = 4
+QUADRANT = 32
 HALF = J // 2
 QUARTER = J // 4
+LEAD = 512
+CLEARED_ON_VECTOR = 512
+CLAMP = 3.4028234663852886e38
 
 
 def by_line(ap, text):
     return ap.rearrange(text, i=4)
+
+
+def half_cols(v):
+    return slice(v * HALF, (v + 1) * HALF)
+
+
+def pair_places(u):
+    return slice(2 * u, 2 * u + 2)
 
 
 def tile_picked_znceg_hinge_po_kernel(tc, x_words, x_scales, hT, label, offs, out_0, out_1, out_2):
@@ -43,33 +55,35 @@ def tile_picked_znceg_hinge_po_kernel(tc, x_words, x_scales, hT, label, offs, ou
         offsets = sb.tile([P, S // 16], U16, name="offsets")
         word_table = sb.tile([P, T], I32, name="word_table", align_bytes=64)
         scale_table = sb.tile([P, T], U8, name="scale_table", align_bytes=64)
-        h_raw = [sb.tile([P, PACK, HALF], F32, name=f"h_raw{i}", align_bytes=64) for i in range(2)]
+        h_raw = [sb.tile([P, PACK, HALF], F32, name=f"h_raw{v}", align_bytes=64) for v in range(2)]
         label_first = sb.tile([P, 2, J], F32, name="label_first", align_bytes=64)
         label_second = [sb.tile([P, 2, HALF], F32, name=f"label_second{v}", align_bytes=64) for v in range(2)]
 
-        def load_h(i):
-            nc.sync.dma_start(h_raw[i][:], h_rows[:, :, i * HALF : (i + 1) * HALF])
+        nc.vector.memset(scale_table[:, :CLEARED_ON_VECTOR].bitcast(I32), 0)
+        nc.gpsimd.memset(scale_table[:, CLEARED_ON_VECTOR:].bitcast(I32), 0)
 
-        nc.vector.memset(scale_table[:, : T - 1536].bitcast(I32), 0)
-        nc.gpsimd.memset(scale_table[:, T - 1536 :].bitcast(I32), 0)
         nc.sync.dma_start(offsets[:], offs)
-        nc.sync.dma_start(word_table[:, 0:512], x_words_i32[:, 0:512])
+        nc.sync.dma_start(word_table[:, 0:LEAD], x_words_i32[:, 0:LEAD])
         for r in range(PACK):
-            nc.sync.dma_start(scale_table[r:P:32, :].bitcast(I32), x_scales_i32[r])
-        nc.sync.dma_start(word_table[:, 512:T], x_words_i32[:, 512:T])
-        load_h(0)
-        load_h(1)
-        nc.sync.dma_start(label_first[:], label_rows[:, 0:2, :])
+            nc.sync.dma_start(scale_table[r:P:QUADRANT, :].bitcast(I32), x_scales_i32[r])
+        nc.sync.dma_start(word_table[:, LEAD:T], x_words_i32[:, LEAD:T])
         for v in range(2):
-            nc.sync.dma_start(label_second[v][:], label_rows[:, 2:4, v * HALF : (v + 1) * HALF])
+            nc.sync.dma_start(h_raw[v][:], h_rows[:, :, half_cols(v)])
+        nc.sync.dma_start(label_first[:], label_rows[:, pair_places(0), :])
+        for v in range(2):
+            nc.sync.dma_start(label_second[v][:], label_rows[:, pair_places(1), half_cols(v)])
 
-        picked_scales = sb.tile([P, S], U8, name="picked_scales", align_bytes=64)
+        picked_scales = [sb.tile([P, S // 2], U8, name=f"picked_scales{g}", align_bytes=64) for g in range(2)]
         dealt_scales = sb.tile([P, PACK, P], U8, name="dealt_scales", align_bytes=64)
         dealt_words = sb.tile([P, PACK, P], U32, name="dealt_words", align_bytes=64)
-        nc.vector.tensor_copy(picked_scales[:], scale_table[:].indirect(offsets[:]))
-        nc.vector.tensor_copy(
-            dealt_scales[:].rearrange("p t m -> p m t"), picked_scales[:].rearrange("p (m t) -> p m t", t=PACK)
-        )
+        for g in range(2):
+            entries = offsets[:, g * (S // 32) : (g + 1) * (S // 32)]
+            nc.vector.tensor_copy(picked_scales[g][:], scale_table[:].indirect(entries))
+        for g in range(2):
+            nc.vector.tensor_copy(
+                dealt_scales[:, :, g * (P // 2) : (g + 1) * (P // 2)].rearrange("p t m -> p m t"),
+                picked_scales[g][:].rearrange("p (m t) -> p m t", t=PACK),
+            )
         nc.vector.tensor_copy(dealt_words[:].rearrange("p t m -> p m t"), word_table[:].bitcast(U32).indirect(offsets[:]))
 
         h_bf = {}
@@ -80,15 +94,12 @@ def tile_picked_znceg_hinge_po_kernel(tc, x_words, x_scales, hT, label, offs, ou
         out_scales = sb.tile([P, J], U8, name="out_scales", align_bytes=64)
         acc = [[psum.tile([P, 2, HALF], F32, name=f"acc{u}{v}") for v in range(2)] for u in range(2)]
 
-        def cast_h(q, on_vector):
+        def round_h(q, copy):
             v, c0 = divmod(q * QUARTER, HALF)
             h_bf[q] = ring.tile([P, QUARTER, PACK], BF16, name="h_bf", align_bytes=64)
             dst = by_line(h_bf[q][:], "p (c i) t -> p c t i")
             src = by_line(h_raw[v][:, :, c0 : c0 + QUARTER], "p t (c i) -> p c t i")
-            if on_vector:
-                nc.vector.tensor_copy(dst, src)
-            else:
-                nc.scalar.copy(dst, src)
+            copy(dst, src)
 
         def product(q):
             v, c0 = divmod(q * QUARTER, HALF)
@@ -111,64 +122,61 @@ def tile_picked_znceg_hinge_po_kernel(tc, x_words, x_scales, hT, label, offs, ou
                 )
 
         def add_label(u, v):
-            part = label_second[v][:] if u else label_first[:, :, v * HALF : (v + 1) * HALF]
-            nc.vector.tensor_tensor(margin[v][:, 2 * u : 2 * u + 2, :], acc[u][v][:], part, ALU.add)
+            part = label_second[v][:] if u else label_first[:, :, half_cols(v)]
+            nc.vector.tensor_tensor(margin[v][:, pair_places(u), :], acc[u][v][:], part, ALU.add)
 
-        def hinge(u, v, engine, store):
+        def store_hinge(u, v):
+            nc.sync.dma_start(out_rows[:, pair_places(u), half_cols(v)], hinge_sb[u][v][:])
+
+        def hinge_shared(u, v):
             dst = hinge_sb[u][v][:]
-            src = margin[v][:, 2 * u : 2 * u + 2, :]
-            if engine == "s":
-                nc.scalar.activation(dst, src, RELU)
-            elif engine == "v":
-                nc.vector.tensor_scalar_max(dst, src, 0.0)
-            else:
-                nc.scalar.activation(dst[:, 0, :], src[:, 0, :], RELU)
-                nc.gpsimd.tensor_scalar(dst[:, 1, :], src[:, 1, :], 3.0e38, 0.0, ALU.min, ALU.max)
-            if store:
-                nc.sync.dma_start(out_rows[:, 2 * u : 2 * u + 2, v * HALF : (v + 1) * HALF], dst)
+            src = margin[v][:, pair_places(u), :]
+            nc.scalar.activation(dst[:, 0, :], src[:, 0, :], RELU)
+            nc.gpsimd.tensor_scalar(dst[:, 1, :], src[:, 1, :], CLAMP, 0.0, ALU.min, ALU.max)
+            store_hinge(u, v)
 
-        def round_out(q, on_vector):
+        def hinge_on_vector(u, v):
+            nc.vector.tensor_scalar_max(hinge_sb[u][v][:], margin[v][:, pair_places(u), :], 0.0)
+            store_hinge(u, v)
+
+        def out_views(q):
             v, c0 = divmod(q * QUARTER, HALF)
             dst = by_line(hinge_bf[v][:, c0 : c0 + QUARTER, :], "p (c i) t -> p c t i")
             src = by_line(margin[v][:, :, c0 : c0 + QUARTER], "p t (c i) -> p c t i")
-            if on_vector:
-                nc.vector.tensor_scalar_max(dst, src, 0.0)
-            else:
-                nc.scalar.activation(dst, src, RELU)
+            return dst, src
 
-        def quantise_out(q0, q1):
-            v, c0 = divmod(q0 * QUARTER, HALF)
-            a, b = q0 * QUARTER, q1 * QUARTER
+        def quantise_out(v):
             nc.vector.quantize_mx(
-                out=out_codes[:, a:b].bitcast(FP8X4),
-                scales=out_scales[:, a:b],
-                in_=hinge_bf[v][:, c0 : c0 + b - a, :].rearrange("p c t -> p (c t)"),
+                out=out_codes[:, half_cols(v)].bitcast(FP8X4),
+                scales=out_scales[:, half_cols(v)],
+                in_=hinge_bf[v][:].rearrange("p c t -> p (c t)"),
             )
-            if b % HALF == 0:
-                nc.sync.dma_start(out_words_i32[:, b - HALF : b], out_codes[:, b - HALF : b])
+            nc.sync.dma_start(out_words_i32[:, half_cols(v)], out_codes[:, half_cols(v)])
 
-        cast_h(0, False)
-        product(0)
-        cast_h(1, False)
-        product(1)
-        cast_h(2, False)
-        cast_h(3, True)
+        for q in range(2):
+            round_h(q, nc.scalar.copy)
+            product(q)
+        round_h(2, nc.scalar.copy)
+        round_h(3, nc.vector.tensor_copy)
         product(3)
         product(2)
-        add_label(0, 0)
-        hinge(0, 0, "g", True)
-        add_label(1, 0)
-        hinge(1, 0, "g", True)
-        round_out(0, False)
+
+        for u in range(2):
+            add_label(u, 0)
+            hinge_shared(u, 0)
+        nc.scalar.activation(*out_views(0), RELU)
         add_label(0, 1)
-        hinge(0, 1, "g", True)
-        round_out(1, False)
-        add_label(1, 1)
-        hinge(1, 1, "v", True)
-        round_out(2, True)
-        round_out(3, True)
-        quantise_out(0, 2)
-        quantise_out(2, 4)
+        hinge_shared(0, 1)
+        nc.scalar.activation(*out_views(1), RELU)
+        for c0 in (0, QUARTER):
+            cols = slice(c0, c0 + QUARTER)
+            nc.vector.tensor_tensor(margin[1][:, pair_places(1), cols], acc[1][1][:, :, cols], label_second[1][:, :, cols], ALU.add)
+        nc.vector.tensor_scalar_max(*out_views(2), 0.0)
+        hinge_on_vector(1, 1)
+        nc.vector.tensor_scalar_max(*out_views(3), 0.0)
+        for v in range(2):
+            quantise_out(v)
+
         for r in range(PACK):
             queue = nc.scalar if r % 2 == 0 else nc.sync
-            queue.dma_start(out_scales_i32[r], out_scales[r:P:32, :].bitcast(I32))
+            queue.dma_start(out_scales_i32[r], out_scales[r:P:QUADRANT, :].bitcast(I32))

@@ -20,7 +20,7 @@ PACK = 4
 QUADRANT = 32
 HALF = J // 2
 QUARTER = J // 4
-LEAD = 512
+LEAD = 768
 CLEARED_ON_VECTOR = 512
 CLAMP = 3.4028234663852886e38
 
@@ -62,8 +62,8 @@ def tile_picked_znceg_hinge_po_kernel(tc, x_words, x_scales, hT, label, offs, ou
         nc.vector.memset(scale_table[:, :CLEARED_ON_VECTOR].bitcast(I32), 0)
         nc.gpsimd.memset(scale_table[:, CLEARED_ON_VECTOR:].bitcast(I32), 0)
 
-        nc.sync.dma_start(offsets[:], offs)
         nc.sync.dma_start(word_table[:, 0:LEAD], x_words_i32[:, 0:LEAD])
+        nc.sync.dma_start(offsets[:], offs)
         for r in range(PACK):
             nc.sync.dma_start(scale_table[r:P:QUADRANT, :].bitcast(I32), x_scales_i32[r])
         nc.sync.dma_start(word_table[:, LEAD:T], x_words_i32[:, LEAD:T])
@@ -81,8 +81,8 @@ def tile_picked_znceg_hinge_po_kernel(tc, x_words, x_scales, hT, label, offs, ou
             nc.vector.tensor_copy(picked_scales[g][:], scale_table[:].indirect(entries))
         for g in range(2):
             nc.vector.tensor_copy(
-                dealt_scales[:, :, g * (P // 2) : (g + 1) * (P // 2)].rearrange("p t m -> p m t"),
-                picked_scales[g][:].rearrange("p (m t) -> p m t", t=PACK),
+                dealt_scales[:, :, g * (P // 2) : (g + 1) * (P // 2)],
+                picked_scales[g][:].rearrange("p (m t) -> p t m", t=PACK),
             )
         nc.vector.tensor_copy(dealt_words[:].rearrange("p t m -> p m t"), word_table[:].bitcast(U32).indirect(offsets[:]))
 
@@ -101,8 +101,9 @@ def tile_picked_znceg_hinge_po_kernel(tc, x_words, x_scales, hT, label, offs, ou
             src = by_line(h_raw[v][:, :, c0 : c0 + QUARTER], "p t (c i) -> p c t i")
             copy(dst, src)
 
-        def product(q):
-            v, c0 = divmod(q * QUARTER, HALF)
+        h_mx = {}
+
+        def quantise_h(q):
             codes = sb.tile([P, QUARTER], U32, name=f"h_codes{q}", align_bytes=64)
             scales = sb.tile([P, QUARTER], U8, name=f"h_scales{q}", align_bytes=64)
             nc.vector.quantize_mx(
@@ -110,9 +111,14 @@ def tile_picked_znceg_hinge_po_kernel(tc, x_words, x_scales, hT, label, offs, ou
                 scales=scales[:],
                 in_=h_bf[q][:].rearrange("p c t -> p (c t)"),
             )
-            for t in range(PACK):
+            h_mx[q] = (codes, scales)
+
+        def product(q, u):
+            v, c0 = divmod(q * QUARTER, HALF)
+            codes, scales = h_mx[q]
+            for t in (2 * u, 2 * u + 1):
                 nc.tensor.matmul_mx(
-                    out=acc[t // 2][v][:, t % 2, c0 : c0 + QUARTER],
+                    out=acc[u][v][:, t % 2, c0 : c0 + QUARTER],
                     lhsT=dealt_words[:, t, :].bitcast(FP8X4),
                     lhsT_scale=dealt_scales[:, t, :],
                     rhs=codes[:].bitcast(FP8X4),
@@ -155,11 +161,16 @@ def tile_picked_znceg_hinge_po_kernel(tc, x_words, x_scales, hT, label, offs, ou
 
         for q in range(2):
             round_h(q, nc.scalar.copy)
-            product(q)
+            quantise_h(q)
+            for u in range(2):
+                product(q, u)
         round_h(2, nc.scalar.copy)
         round_h(3, nc.vector.tensor_copy)
-        product(3)
-        product(2)
+        quantise_h(3)
+        quantise_h(2)
+        for u in range(2):
+            product(3, u)
+            product(2, u)
 
         for u in range(2):
             add_label(u, 0)

@@ -20,8 +20,7 @@ PACK = 4
 QUADRANT = 32
 HALF = J // 2
 QUARTER = J // 4
-LEAD = 768
-CLEARED_ON_VECTOR = 512
+LEAD = 640
 CLAMP = 3.4028234663852886e38
 
 
@@ -59,8 +58,7 @@ def tile_picked_znceg_hinge_po_kernel(tc, x_words, x_scales, hT, label, offs, ou
         label_first = sb.tile([P, 2, J], F32, name="label_first", align_bytes=64)
         label_second = [sb.tile([P, 2, HALF], F32, name=f"label_second{v}", align_bytes=64) for v in range(2)]
 
-        nc.vector.memset(scale_table[:, :CLEARED_ON_VECTOR].bitcast(I32), 0)
-        nc.gpsimd.memset(scale_table[:, CLEARED_ON_VECTOR:].bitcast(I32), 0)
+        nc.vector.memset(scale_table[:].bitcast(I32), 0)
 
         nc.sync.dma_start(word_table[:, 0:LEAD], x_words_i32[:, 0:LEAD])
         nc.sync.dma_start(offsets[:], offs)

@@ -20,7 +20,7 @@ PACK = 4
 QUADRANT = 32
 HALF = J // 2
 QUARTER = J // 4
-LEAD = 640
+STAGE = 112
 CLAMP = 3.4028234663852886e38
 
 
@@ -42,36 +42,29 @@ def tile_picked_znceg_hinge_po_kernel(tc, x_words, x_scales, hT, label, offs, ou
     label_rows = label.rearrange("(p t) j -> p t j", t=PACK)
     out_rows = out_0.rearrange("(p t) j -> p t j", t=PACK)
     x_words_i32 = x_words[0].rearrange("p c t -> p (c t)").bitcast(I32)
-    x_scales_i32 = x_scales[0].bitcast(I32).rearrange("(q r) c -> r q c", r=PACK)
+    x_scales_i32 = x_scales[0].bitcast(I32)
     out_words_i32 = out_1[0].rearrange("p c t -> p (c t)").bitcast(I32)
     out_scales_i32 = out_2[0].bitcast(I32).rearrange("(q r) c -> r q c", r=PACK)
 
     with ExitStack() as ctx:
         sb = ctx.enter_context(tc.tile_pool(name="sb", bufs=1))
-        ring = ctx.enter_context(tc.tile_pool(name="ring", bufs=3))
+        reuse = ctx.enter_context(tc.tile_pool(name="reuse", bufs=1))
         psum = ctx.enter_context(tc.psum_pool(name="psum", bufs=1))
 
         offsets = sb.tile([P, S // 16], U16, name="offsets")
-        word_table = sb.tile([P, T], I32, name="word_table", align_bytes=64)
+        word_table = reuse.tile([P, T], I32, name="word_table", offset=4096)
         scale_table = sb.tile([P, T], U8, name="scale_table", align_bytes=64)
         h_raw = [sb.tile([P, PACK, HALF], F32, name=f"h_raw{v}", align_bytes=64) for v in range(2)]
-        label_first = sb.tile([P, 2, J], F32, name="label_first", align_bytes=64)
-        label_second = [sb.tile([P, 2, HALF], F32, name=f"label_second{v}", align_bytes=64) for v in range(2)]
 
-        nc.vector.memset(scale_table[:].bitcast(I32), 0)
+        nc.vector.memset(scale_table[0:STAGE, :].bitcast(I32), 0)
 
-        nc.sync.dma_start(word_table[:, 0:LEAD], x_words_i32[:, 0:LEAD])
+        nc.sync.dma_start(scale_table[STAGE:P, :].bitcast(I32), x_scales_i32)
         nc.sync.dma_start(offsets[:], offs)
-        for r in range(PACK):
-            nc.sync.dma_start(scale_table[r:P:QUADRANT, :].bitcast(I32), x_scales_i32[r])
-        nc.sync.dma_start(word_table[:, LEAD:T], x_words_i32[:, LEAD:T])
+        nc.sync.dma_start(word_table[:], x_words_i32)
         for v in range(2):
             nc.sync.dma_start(h_raw[v][:], h_rows[:, :, half_cols(v)])
-        nc.sync.dma_start(label_first[:], label_rows[:, pair_places(0), :])
-        for v in range(2):
-            nc.sync.dma_start(label_second[v][:], label_rows[:, pair_places(1), half_cols(v)])
 
-        picked_scales = [sb.tile([P, S // 2], U8, name=f"picked_scales{g}", align_bytes=64) for g in range(2)]
+        picked_scales = [reuse.tile([P, S // 2], U8, name=f"picked_scales{g}", offset=(12288, 1920)[g]) for g in range(2)]
         dealt_scales = sb.tile([P, PACK, P], U8, name="dealt_scales", align_bytes=64)
         dealt_words = sb.tile([P, PACK, P], U32, name="dealt_words", align_bytes=64)
         for g in range(2):
@@ -82,9 +75,16 @@ def tile_picked_znceg_hinge_po_kernel(tc, x_words, x_scales, hT, label, offs, ou
                 dealt_scales[:, :, g * (P // 2) : (g + 1) * (P // 2)],
                 picked_scales[g][:].rearrange("p (m t) -> p t m", t=PACK),
             )
+        dealt_rows = dealt_scales[:].rearrange("p t m -> p (t m)")
+        for r in range(PACK):
+            nc.sync.dma_start(dealt_rows[r:STAGE:QUADRANT, :].bitcast(I32), dealt_rows[STAGE + r : P : PACK, :].bitcast(I32))
+        label_sb = [[reuse.tile([P, 2, HALF], F32, name=f"label{u}{v}", offset=2048 * (2 * v + u)) for v in range(2)] for u in range(2)]
+        for u in range(2):
+            nc.sync.dma_start(label_sb[u][0][:], label_rows[:, pair_places(u), half_cols(0)])
         nc.vector.tensor_copy(dealt_words[:].rearrange("p t m -> p m t"), word_table[:].bitcast(U32).indirect(offsets[:]))
+        for u in range(2):
+            nc.sync.dma_start(label_sb[u][1][:], label_rows[:, pair_places(u), half_cols(1)])
 
-        h_bf = {}
         margin = [sb.tile([P, PACK, HALF], F32, name=f"margin{v}", align_bytes=64) for v in range(2)]
         hinge_bf = [sb.tile([P, HALF, PACK], BF16, name=f"hinge_bf{v}", align_bytes=64) for v in range(2)]
         hinge_sb = [[sb.tile([P, 2, HALF], F32, name=f"hinge{u}{v}", align_bytes=64) for v in range(2)] for u in range(2)]
@@ -92,31 +92,17 @@ def tile_picked_znceg_hinge_po_kernel(tc, x_words, x_scales, hT, label, offs, ou
         out_scales = sb.tile([P, J], U8, name="out_scales", align_bytes=64)
         acc = [[psum.tile([P, 2, HALF], F32, name=f"acc{u}{v}") for v in range(2)] for u in range(2)]
 
-        def round_h(q, copy):
-            v, c0 = divmod(q * QUARTER, HALF)
-            h_bf[q] = ring.tile([P, QUARTER, PACK], BF16, name="h_bf", align_bytes=64)
-            dst = by_line(h_bf[q][:], "p (c i) t -> p c t i")
-            src = by_line(h_raw[v][:, :, c0 : c0 + QUARTER], "p t (c i) -> p c t i")
-            copy(dst, src)
-
-        h_mx = {}
-
-        def quantise_h(q):
-            codes = sb.tile([P, QUARTER], U32, name=f"h_codes{q}", align_bytes=64)
-            scales = sb.tile([P, QUARTER], U8, name=f"h_scales{q}", align_bytes=64)
-            nc.vector.quantize_mx(
-                out=codes[:].bitcast(FP8X4),
-                scales=scales[:],
-                in_=h_bf[q][:].rearrange("p c t -> p (c t)"),
-            )
-            h_mx[q] = (codes, scales)
-
-        def product(q, u):
-            v, c0 = divmod(q * QUARTER, HALF)
-            codes, scales = h_mx[q]
-            for t in (2 * u, 2 * u + 1):
+        def quantise_and_multiply(v):
+            h_bf = sb.tile([P, HALF, PACK], BF16, name="h_bf", align_bytes=64)
+            for c0, copy in ((0, nc.scalar.copy), (QUARTER, nc.vector.tensor_copy)):
+                cols = slice(c0, c0 + QUARTER)
+                copy(by_line(h_bf[:, cols, :], "p (c i) t -> p c t i"), by_line(h_raw[v][:, :, cols], "p t (c i) -> p c t i"))
+            codes = sb.tile([P, HALF], U32, name=f"h_codes{v}", align_bytes=64)
+            scales = sb.tile([P, HALF], U8, name=f"h_scales{v}", align_bytes=64)
+            nc.vector.quantize_mx(out=codes[:].bitcast(FP8X4), scales=scales[:], in_=h_bf[:].rearrange("p c t -> p (c t)"))
+            for t in range(PACK):
                 nc.tensor.matmul_mx(
-                    out=acc[u][v][:, t % 2, c0 : c0 + QUARTER],
+                    out=acc[t // 2][v][:, t % 2, :],
                     lhsT=dealt_words[:, t, :].bitcast(FP8X4),
                     lhsT_scale=dealt_scales[:, t, :],
                     rhs=codes[:].bitcast(FP8X4),
@@ -126,8 +112,7 @@ def tile_picked_znceg_hinge_po_kernel(tc, x_words, x_scales, hT, label, offs, ou
                 )
 
         def add_label(u, v):
-            part = label_second[v][:] if u else label_first[:, :, half_cols(v)]
-            nc.vector.tensor_tensor(margin[v][:, pair_places(u), :], acc[u][v][:], part, ALU.add)
+            nc.vector.tensor_tensor(margin[v][:, pair_places(u), :], acc[u][v][:], label_sb[u][v][:], ALU.add)
 
         def store_hinge(u, v):
             nc.sync.dma_start(out_rows[:, pair_places(u), half_cols(v)], hinge_sb[u][v][:])
@@ -157,18 +142,8 @@ def tile_picked_znceg_hinge_po_kernel(tc, x_words, x_scales, hT, label, offs, ou
             )
             nc.sync.dma_start(out_words_i32[:, half_cols(v)], out_codes[:, half_cols(v)])
 
-        for q in range(2):
-            round_h(q, nc.scalar.copy)
-            quantise_h(q)
-            for u in range(2):
-                product(q, u)
-        round_h(2, nc.scalar.copy)
-        round_h(3, nc.vector.tensor_copy)
-        quantise_h(3)
-        quantise_h(2)
-        for u in range(2):
-            product(3, u)
-            product(2, u)
+        for v in range(2):
+            quantise_and_multiply(v)
 
         for u in range(2):
             add_label(u, 0)
@@ -179,7 +154,7 @@ def tile_picked_znceg_hinge_po_kernel(tc, x_words, x_scales, hT, label, offs, ou
         nc.scalar.activation(*out_views(1), RELU)
         for c0 in (0, QUARTER):
             cols = slice(c0, c0 + QUARTER)
-            nc.vector.tensor_tensor(margin[1][:, pair_places(1), cols], acc[1][1][:, :, cols], label_second[1][:, :, cols], ALU.add)
+            nc.vector.tensor_tensor(margin[1][:, pair_places(1), cols], acc[1][1][:, :, cols], label_sb[1][1][:, :, cols], ALU.add)
         nc.vector.tensor_scalar_max(*out_views(2), 0.0)
         hinge_on_vector(1, 1)
         nc.vector.tensor_scalar_max(*out_views(3), 0.0)

@@ -48,6 +48,7 @@ def tile_picked_znceg_hinge_po_kernel(tc, x_words, x_scales, hT, label, offs, ou
 
     with ExitStack() as ctx:
         sb = ctx.enter_context(tc.tile_pool(name="sb", bufs=1))
+        ring = ctx.enter_context(tc.tile_pool(name="ring", bufs=1))
         reuse = ctx.enter_context(tc.tile_pool(name="reuse", bufs=1))
         psum = ctx.enter_context(tc.psum_pool(name="psum", bufs=1))
 
@@ -93,13 +94,16 @@ def tile_picked_znceg_hinge_po_kernel(tc, x_words, x_scales, hT, label, offs, ou
         acc = [[psum.tile([P, 2, HALF], F32, name=f"acc{u}{v}") for v in range(2)] for u in range(2)]
 
         def quantise_and_multiply(v):
-            h_bf = sb.tile([P, HALF, PACK], BF16, name="h_bf", align_bytes=64)
-            for c0, copy in ((0, nc.scalar.copy), (QUARTER, nc.vector.tensor_copy)):
-                cols = slice(c0, c0 + QUARTER)
-                copy(by_line(h_bf[:, cols, :], "p (c i) t -> p c t i"), by_line(h_raw[v][:, :, cols], "p t (c i) -> p c t i"))
             codes = sb.tile([P, HALF], U32, name=f"h_codes{v}", align_bytes=64)
             scales = sb.tile([P, HALF], U8, name=f"h_scales{v}", align_bytes=64)
-            nc.vector.quantize_mx(out=codes[:].bitcast(FP8X4), scales=scales[:], in_=h_bf[:].rearrange("p c t -> p (c t)"))
+            rounded = []
+            for c0, copy in ((0, nc.scalar.copy), (QUARTER, nc.vector.tensor_copy)):
+                cols = slice(c0, c0 + QUARTER)
+                h_bf = ring.tile([P, QUARTER, PACK], BF16, name=f"h_bf{v}{c0}", align_bytes=64, offset=(0, 1024, 2048, 512)[2 * v + c0 // QUARTER])
+                copy(by_line(h_bf[:], "p (c i) t -> p c t i"), by_line(h_raw[v][:, :, cols], "p t (c i) -> p c t i"))
+                rounded.append((cols, h_bf))
+            for cols, h_bf in rounded:
+                nc.vector.quantize_mx(out=codes[:, cols].bitcast(FP8X4), scales=scales[:, cols], in_=h_bf[:].rearrange("p c t -> p (c t)"))
             for t in range(PACK):
                 nc.tensor.matmul_mx(
                     out=acc[t // 2][v][:, t % 2, :],
@@ -124,23 +128,19 @@ def tile_picked_znceg_hinge_po_kernel(tc, x_words, x_scales, hT, label, offs, ou
             nc.gpsimd.tensor_scalar(dst[:, 1, :], src[:, 1, :], CLAMP, 0.0, ALU.min, ALU.max)
             store_hinge(u, v)
 
-        def hinge_on_vector(u, v):
-            nc.vector.tensor_scalar_max(hinge_sb[u][v][:], margin[v][:, pair_places(u), :], 0.0)
-            store_hinge(u, v)
-
         def out_views(q):
             v, c0 = divmod(q * QUARTER, HALF)
             dst = by_line(hinge_bf[v][:, c0 : c0 + QUARTER, :], "p (c i) t -> p c t i")
             src = by_line(margin[v][:, :, c0 : c0 + QUARTER], "p t (c i) -> p c t i")
             return dst, src
 
-        def quantise_out(v):
+        def quantise_out(c0, width):
+            v, c = divmod(c0, HALF)
             nc.vector.quantize_mx(
-                out=out_codes[:, half_cols(v)].bitcast(FP8X4),
-                scales=out_scales[:, half_cols(v)],
-                in_=hinge_bf[v][:].rearrange("p c t -> p (c t)"),
+                out=out_codes[:, c0 : c0 + width].bitcast(FP8X4),
+                scales=out_scales[:, c0 : c0 + width],
+                in_=hinge_bf[v][:, c : c + width, :].rearrange("p c t -> p (c t)"),
             )
-            nc.sync.dma_start(out_words_i32[:, half_cols(v)], out_codes[:, half_cols(v)])
 
         for v in range(2):
             quantise_and_multiply(v)
@@ -155,11 +155,17 @@ def tile_picked_znceg_hinge_po_kernel(tc, x_words, x_scales, hT, label, offs, ou
         for c0 in (0, QUARTER):
             cols = slice(c0, c0 + QUARTER)
             nc.vector.tensor_tensor(margin[1][:, pair_places(1), cols], acc[1][1][:, :, cols], label_sb[1][1][:, :, cols], ALU.add)
-        nc.vector.tensor_scalar_max(*out_views(2), 0.0)
-        hinge_on_vector(1, 1)
+        for c0 in (0, QUARTER):
+            cols = slice(c0, c0 + QUARTER)
+            nc.vector.tensor_scalar_max(hinge_sb[1][1][:, :, cols], margin[1][:, pair_places(1), cols], 0.0)
+        store_hinge(1, 1)
+        nc.scalar.activation(*out_views(2), RELU)
         nc.vector.tensor_scalar_max(*out_views(3), 0.0)
-        for v in range(2):
-            quantise_out(v)
+        quantise_out(0, HALF)
+        nc.sync.dma_start(out_words_i32[:, half_cols(0)], out_codes[:, half_cols(0)])
+        quantise_out(HALF + QUARTER, QUARTER)
+        quantise_out(HALF, QUARTER)
+        nc.sync.dma_start(out_words_i32[:, half_cols(1)], out_codes[:, half_cols(1)])
 
         for r in range(PACK):
             queue = nc.scalar if r % 2 == 0 else nc.sync

@@ -91,7 +91,8 @@ def tile_picked_znceg_hinge_po_kernel(tc, x_words, x_scales, hT, label, offs, ou
         hinge_sb = [[sb.tile([P, 2, HALF], F32, name=f"hinge{u}{v}", align_bytes=64) for v in range(2)] for u in range(2)]
         out_codes = sb.tile([P, J], I32, name="out_codes", align_bytes=64)
         out_scales = sb.tile([P, J], U8, name="out_scales", align_bytes=64)
-        acc = [[psum.tile([P, 2, HALF], F32, name=f"acc{u}{v}") for v in range(2)] for u in range(2)]
+        acc = {(t, v): psum.tile([P, HALF], F32, name=f"acc{t}{v}") for v in range(2) for t in range(PACK - 2 * v)}
+        acc_last = [psum.tile([P, 2, QUARTER], F32, name=f"acc_last{c}") for c in range(2)]
 
         def quantise_and_multiply(v):
             codes = sb.tile([P, HALF], U32, name=f"h_codes{v}", align_bytes=64)
@@ -104,19 +105,23 @@ def tile_picked_znceg_hinge_po_kernel(tc, x_words, x_scales, hT, label, offs, ou
                 rounded.append((cols, h_bf))
             for cols, h_bf in rounded:
                 nc.vector.quantize_mx(out=codes[:, cols].bitcast(FP8X4), scales=scales[:, cols], in_=h_bf[:].rearrange("p c t -> p (c t)"))
-            for t in range(PACK):
+            passes = [(acc[t, v][:], t, slice(0, HALF)) for t in range(PACK - 2 * v)]
+            if v:
+                passes += [(acc_last[c][:, t - 2, :], t, slice(c * QUARTER, (c + 1) * QUARTER)) for c in range(2) for t in (2, 3)]
+            for out, t, cols in passes:
                 nc.tensor.matmul_mx(
-                    out=acc[t // 2][v][:, t % 2, :],
+                    out=out,
                     lhsT=dealt_words[:, t, :].bitcast(FP8X4),
                     lhsT_scale=dealt_scales[:, t, :],
-                    rhs=codes[:].bitcast(FP8X4),
-                    rhs_scale=scales[:],
+                    rhs=codes[:, cols].bitcast(FP8X4),
+                    rhs_scale=scales[:, cols],
                     start=True,
                     stop=True,
                 )
 
         def add_label(u, v):
-            nc.vector.tensor_tensor(margin[v][:, pair_places(u), :], acc[u][v][:], label_sb[u][v][:], ALU.add)
+            for t in (2 * u, 2 * u + 1):
+                nc.vector.tensor_tensor(margin[v][:, t, :], acc[t, v][:], label_sb[u][v][:, t % 2, :], ALU.add)
 
         def store_hinge(u, v):
             nc.sync.dma_start(out_rows[:, pair_places(u), half_cols(v)], hinge_sb[u][v][:])
@@ -124,14 +129,14 @@ def tile_picked_znceg_hinge_po_kernel(tc, x_words, x_scales, hT, label, offs, ou
         def hinge_shared(u, v):
             dst = hinge_sb[u][v][:]
             src = margin[v][:, pair_places(u), :]
-            nc.scalar.activation(dst[:, 0, :], src[:, 0, :], RELU)
-            nc.gpsimd.tensor_scalar(dst[:, 1, :], src[:, 1, :], CLAMP, 0.0, ALU.min, ALU.max)
+            nc.gpsimd.tensor_scalar(dst[:, 0, :], src[:, 0, :], CLAMP, 0.0, ALU.min, ALU.max)
+            nc.scalar.activation(dst[:, 1, :], src[:, 1, :], RELU)
             store_hinge(u, v)
 
-        def out_views(q):
-            v, c0 = divmod(q * QUARTER, HALF)
-            dst = by_line(hinge_bf[v][:, c0 : c0 + QUARTER, :], "p (c i) t -> p c t i")
-            src = by_line(margin[v][:, :, c0 : c0 + QUARTER], "p t (c i) -> p c t i")
+        def out_views(c0, width):
+            v, c = divmod(c0, HALF)
+            dst = by_line(hinge_bf[v][:, c : c + width, :], "p (c i) t -> p c t i")
+            src = by_line(margin[v][:, :, c : c + width], "p t (c i) -> p c t i")
             return dst, src
 
         def quantise_out(c0, width):
@@ -148,23 +153,22 @@ def tile_picked_znceg_hinge_po_kernel(tc, x_words, x_scales, hT, label, offs, ou
         for u in range(2):
             add_label(u, 0)
             hinge_shared(u, 0)
-        nc.scalar.activation(*out_views(0), RELU)
+        nc.scalar.activation(*out_views(0, QUARTER), RELU)
         add_label(0, 1)
         hinge_shared(0, 1)
-        nc.scalar.activation(*out_views(1), RELU)
+        nc.scalar.activation(*out_views(QUARTER, QUARTER), RELU)
         for c0 in (0, QUARTER):
             cols = slice(c0, c0 + QUARTER)
-            nc.vector.tensor_tensor(margin[1][:, pair_places(1), cols], acc[1][1][:, :, cols], label_sb[1][1][:, :, cols], ALU.add)
-        for c0 in (0, QUARTER):
-            cols = slice(c0, c0 + QUARTER)
-            nc.vector.tensor_scalar_max(hinge_sb[1][1][:, :, cols], margin[1][:, pair_places(1), cols], 0.0)
+            nc.vector.tensor_tensor(margin[1][:, pair_places(1), cols], acc_last[c0 // QUARTER][:], label_sb[1][1][:, :, cols], ALU.add)
+        nc.gpsimd.tensor_scalar(hinge_sb[1][1][:, :, 0:QUARTER], margin[1][:, pair_places(1), 0:QUARTER], CLAMP, 0.0, ALU.min, ALU.max)
+        nc.vector.tensor_scalar_max(*out_views(HALF, QUARTER), 0.0)
+        nc.vector.tensor_scalar_max(hinge_sb[1][1][:, :, QUARTER:HALF], margin[1][:, pair_places(1), QUARTER:HALF], 0.0)
         store_hinge(1, 1)
-        nc.scalar.activation(*out_views(2), RELU)
-        nc.vector.tensor_scalar_max(*out_views(3), 0.0)
+        nc.scalar.activation(*out_views(J - 64, 64), RELU)
+        nc.vector.tensor_scalar_max(*out_views(HALF + QUARTER, 64), 0.0)
         quantise_out(0, HALF)
         nc.sync.dma_start(out_words_i32[:, half_cols(0)], out_codes[:, half_cols(0)])
-        quantise_out(HALF + QUARTER, QUARTER)
-        quantise_out(HALF, QUARTER)
+        quantise_out(HALF, HALF)
         nc.sync.dma_start(out_words_i32[:, half_cols(1)], out_codes[:, half_cols(1)])
 
         for r in range(PACK):

@@ -20,6 +20,7 @@ PACK = 4
 QUADRANT = 32
 HALF = J // 2
 QUARTER = J // 4
+LEAD = 256
 STAGE = 112
 CLAMP = 3.4028234663852886e38
 
@@ -59,9 +60,10 @@ def tile_picked_znceg_hinge_po_kernel(tc, x_words, x_scales, hT, label, offs, ou
 
         nc.vector.memset(scale_table[0:STAGE, :].bitcast(I32), 0)
 
+        nc.sync.dma_start(word_table[:, 0:LEAD], x_words_i32[:, 0:LEAD])
         nc.sync.dma_start(scale_table[STAGE:P, :].bitcast(I32), x_scales_i32)
         nc.sync.dma_start(offsets[:], offs)
-        nc.sync.dma_start(word_table[:], x_words_i32)
+        nc.sync.dma_start(word_table[:, LEAD:T], x_words_i32[:, LEAD:T])
         for v in range(2):
             nc.sync.dma_start(h_raw[v][:], h_rows[:, :, half_cols(v)])
 
@@ -129,8 +131,13 @@ def tile_picked_znceg_hinge_po_kernel(tc, x_words, x_scales, hT, label, offs, ou
         def hinge_shared(u, v):
             dst = hinge_sb[u][v][:]
             src = margin[v][:, pair_places(u), :]
-            nc.gpsimd.tensor_scalar(dst[:, 0, :], src[:, 0, :], CLAMP, 0.0, ALU.min, ALU.max)
-            nc.scalar.activation(dst[:, 1, :], src[:, 1, :], RELU)
+            if v == 0:
+                nc.scalar.activation(dst[:, 0, :], src[:, 0, :], RELU)
+                nc.scalar.activation(dst[:, 1, 0:160], src[:, 1, 0:160], RELU)
+                nc.gpsimd.tensor_scalar(dst[:, 1, 160:HALF], src[:, 1, 160:HALF], CLAMP, 0.0, ALU.min, ALU.max)
+            else:
+                nc.gpsimd.tensor_scalar(dst[:, 0, :], src[:, 0, :], CLAMP, 0.0, ALU.min, ALU.max)
+                nc.scalar.activation(dst[:, 1, :], src[:, 1, :], RELU)
             store_hinge(u, v)
 
         def out_views(c0, width):

@@ -20,9 +20,13 @@ PACK = 4
 QUADRANT = 32
 HALF = J // 2
 QUARTER = J // 4
-LEAD = 256
-STAGE = 112
+STAGE = P - K // 32
+SCALAR_HINGE = 160
+SCALAR_TAIL = 64
 CLAMP = 3.4028234663852886e38
+
+LABEL_BYTES = 2 * HALF * 4
+ROUNDED_BYTES = QUARTER * PACK * 2
 
 
 def by_line(ap, text):
@@ -49,25 +53,27 @@ def tile_picked_znceg_hinge_po_kernel(tc, x_words, x_scales, hT, label, offs, ou
 
     with ExitStack() as ctx:
         sb = ctx.enter_context(tc.tile_pool(name="sb", bufs=1))
-        ring = ctx.enter_context(tc.tile_pool(name="ring", bufs=1))
+        rounding = ctx.enter_context(tc.tile_pool(name="rounding", bufs=1))
         reuse = ctx.enter_context(tc.tile_pool(name="reuse", bufs=1))
         psum = ctx.enter_context(tc.psum_pool(name="psum", bufs=1))
 
+        word_table_at = 2 * LABEL_BYTES
+        picked_at = (word_table_at + 4 * T, LABEL_BYTES - S // 4)
+
         offsets = sb.tile([P, S // 16], U16, name="offsets")
-        word_table = reuse.tile([P, T], I32, name="word_table", offset=4096)
+        word_table = reuse.tile([P, T], I32, name="word_table", offset=word_table_at)
         scale_table = sb.tile([P, T], U8, name="scale_table", align_bytes=64)
         h_raw = [sb.tile([P, PACK, HALF], F32, name=f"h_raw{v}", align_bytes=64) for v in range(2)]
 
         nc.vector.memset(scale_table[0:STAGE, :].bitcast(I32), 0)
 
-        nc.sync.dma_start(word_table[:, 0:LEAD], x_words_i32[:, 0:LEAD])
         nc.sync.dma_start(scale_table[STAGE:P, :].bitcast(I32), x_scales_i32)
         nc.sync.dma_start(offsets[:], offs)
-        nc.sync.dma_start(word_table[:, LEAD:T], x_words_i32[:, LEAD:T])
+        nc.sync.dma_start(word_table[:], x_words_i32)
         for v in range(2):
             nc.sync.dma_start(h_raw[v][:], h_rows[:, :, half_cols(v)])
 
-        picked_scales = [reuse.tile([P, S // 2], U8, name=f"picked_scales{g}", offset=(12288, 1920)[g]) for g in range(2)]
+        picked_scales = [reuse.tile([P, S // 2], U8, name=f"picked_scales{g}", offset=picked_at[g]) for g in range(2)]
         dealt_scales = sb.tile([P, PACK, P], U8, name="dealt_scales", align_bytes=64)
         dealt_words = sb.tile([P, PACK, P], U32, name="dealt_words", align_bytes=64)
         for g in range(2):
@@ -81,7 +87,11 @@ def tile_picked_znceg_hinge_po_kernel(tc, x_words, x_scales, hT, label, offs, ou
         dealt_rows = dealt_scales[:].rearrange("p t m -> p (t m)")
         for r in range(PACK):
             nc.sync.dma_start(dealt_rows[r:STAGE:QUADRANT, :].bitcast(I32), dealt_rows[STAGE + r : P : PACK, :].bitcast(I32))
-        label_sb = [[reuse.tile([P, 2, HALF], F32, name=f"label{u}{v}", offset=2048 * (2 * v + u)) for v in range(2)] for u in range(2)]
+
+        label_sb = [
+            [reuse.tile([P, 2, HALF], F32, name=f"label{u}{v}", offset=LABEL_BYTES * (2 * v + u)) for v in range(2)]
+            for u in range(2)
+        ]
         for u in range(2):
             nc.sync.dma_start(label_sb[u][0][:], label_rows[:, pair_places(u), half_cols(0)])
         nc.vector.tensor_copy(dealt_words[:].rearrange("p t m -> p m t"), word_table[:].bitcast(U32).indirect(offsets[:]))
@@ -95,21 +105,26 @@ def tile_picked_znceg_hinge_po_kernel(tc, x_words, x_scales, hT, label, offs, ou
         out_scales = sb.tile([P, J], U8, name="out_scales", align_bytes=64)
         acc = {(t, v): psum.tile([P, HALF], F32, name=f"acc{t}{v}") for v in range(2) for t in range(PACK - 2 * v)}
         acc_last = [psum.tile([P, 2, QUARTER], F32, name=f"acc_last{c}") for c in range(2)]
+        rounded_at = (0, ROUNDED_BYTES, 2 * ROUNDED_BYTES, ROUNDED_BYTES // 2)
 
         def quantise_and_multiply(v):
             codes = sb.tile([P, HALF], U32, name=f"h_codes{v}", align_bytes=64)
             scales = sb.tile([P, HALF], U8, name=f"h_scales{v}", align_bytes=64)
-            rounded = []
-            for c0, copy in ((0, nc.scalar.copy), (QUARTER, nc.vector.tensor_copy)):
-                cols = slice(c0, c0 + QUARTER)
-                h_bf = ring.tile([P, QUARTER, PACK], BF16, name=f"h_bf{v}{c0}", align_bytes=64, offset=(0, 1024, 2048, 512)[2 * v + c0 // QUARTER])
-                copy(by_line(h_bf[:], "p (c i) t -> p c t i"), by_line(h_raw[v][:, :, cols], "p t (c i) -> p c t i"))
-                rounded.append((cols, h_bf))
-            for cols, h_bf in rounded:
-                nc.vector.quantize_mx(out=codes[:, cols].bitcast(FP8X4), scales=scales[:, cols], in_=h_bf[:].rearrange("p c t -> p (c t)"))
+            quarters = [slice(0, QUARTER), slice(QUARTER, HALF)]
+            h_bf = []
+            for c, copy in enumerate((nc.scalar.copy, nc.vector.tensor_copy)):
+                q = 2 * v + c
+                h_bf.append(rounding.tile([P, QUARTER, PACK], BF16, name=f"h_bf{q}", align_bytes=64, offset=rounded_at[q]))
+                copy(by_line(h_bf[c][:], "p (c i) t -> p c t i"), by_line(h_raw[v][:, :, quarters[c]], "p t (c i) -> p c t i"))
+            for c, cols in enumerate(quarters):
+                nc.vector.quantize_mx(
+                    out=codes[:, cols].bitcast(FP8X4),
+                    scales=scales[:, cols],
+                    in_=h_bf[c][:].rearrange("p c t -> p (c t)"),
+                )
             passes = [(acc[t, v][:], t, slice(0, HALF)) for t in range(PACK - 2 * v)]
-            if v:
-                passes += [(acc_last[c][:, t - 2, :], t, slice(c * QUARTER, (c + 1) * QUARTER)) for c in range(2) for t in (2, 3)]
+            if v == 1:
+                passes += [(acc_last[c][:, t - 2, :], t, quarters[c]) for c in range(2) for t in (2, 3)]
             for out, t, cols in passes:
                 nc.tensor.matmul_mx(
                     out=out,
@@ -125,20 +140,11 @@ def tile_picked_znceg_hinge_po_kernel(tc, x_words, x_scales, hT, label, offs, ou
             for t in (2 * u, 2 * u + 1):
                 nc.vector.tensor_tensor(margin[v][:, t, :], acc[t, v][:], label_sb[u][v][:, t % 2, :], ALU.add)
 
+        def hinge_on_gpsimd(dst, src):
+            nc.gpsimd.tensor_scalar(dst, src, CLAMP, 0.0, ALU.min, ALU.max)
+
         def store_hinge(u, v):
             nc.sync.dma_start(out_rows[:, pair_places(u), half_cols(v)], hinge_sb[u][v][:])
-
-        def hinge_shared(u, v):
-            dst = hinge_sb[u][v][:]
-            src = margin[v][:, pair_places(u), :]
-            if v == 0:
-                nc.scalar.activation(dst[:, 0, :], src[:, 0, :], RELU)
-                nc.scalar.activation(dst[:, 1, 0:160], src[:, 1, 0:160], RELU)
-                nc.gpsimd.tensor_scalar(dst[:, 1, 160:HALF], src[:, 1, 160:HALF], CLAMP, 0.0, ALU.min, ALU.max)
-            else:
-                nc.gpsimd.tensor_scalar(dst[:, 0, :], src[:, 0, :], CLAMP, 0.0, ALU.min, ALU.max)
-                nc.scalar.activation(dst[:, 1, :], src[:, 1, :], RELU)
-            store_hinge(u, v)
 
         def out_views(c0, width):
             v, c = divmod(c0, HALF)
@@ -146,37 +152,43 @@ def tile_picked_znceg_hinge_po_kernel(tc, x_words, x_scales, hT, label, offs, ou
             src = by_line(margin[v][:, :, c : c + width], "p t (c i) -> p c t i")
             return dst, src
 
-        def quantise_out(c0, width):
-            v, c = divmod(c0, HALF)
+        def quantise_out(v):
             nc.vector.quantize_mx(
-                out=out_codes[:, c0 : c0 + width].bitcast(FP8X4),
-                scales=out_scales[:, c0 : c0 + width],
-                in_=hinge_bf[v][:, c : c + width, :].rearrange("p c t -> p (c t)"),
+                out=out_codes[:, half_cols(v)].bitcast(FP8X4),
+                scales=out_scales[:, half_cols(v)],
+                in_=hinge_bf[v][:].rearrange("p c t -> p (c t)"),
             )
+            nc.sync.dma_start(out_words_i32[:, half_cols(v)], out_codes[:, half_cols(v)])
 
         for v in range(2):
             quantise_and_multiply(v)
 
         for u in range(2):
             add_label(u, 0)
-            hinge_shared(u, 0)
+            dst, src = hinge_sb[u][0][:], margin[0][:, pair_places(u), :]
+            nc.scalar.activation(dst[:, 0, :], src[:, 0, :], RELU)
+            nc.scalar.activation(dst[:, 1, 0:SCALAR_HINGE], src[:, 1, 0:SCALAR_HINGE], RELU)
+            hinge_on_gpsimd(dst[:, 1, SCALAR_HINGE:HALF], src[:, 1, SCALAR_HINGE:HALF])
+            store_hinge(u, 0)
         nc.scalar.activation(*out_views(0, QUARTER), RELU)
         add_label(0, 1)
-        hinge_shared(0, 1)
+        hinge_on_gpsimd(hinge_sb[0][1][:, 0, :], margin[1][:, 0, :])
+        nc.scalar.activation(hinge_sb[0][1][:, 1, :], margin[1][:, 1, :], RELU)
+        store_hinge(0, 1)
         nc.scalar.activation(*out_views(QUARTER, QUARTER), RELU)
-        for c0 in (0, QUARTER):
-            cols = slice(c0, c0 + QUARTER)
-            nc.vector.tensor_tensor(margin[1][:, pair_places(1), cols], acc_last[c0 // QUARTER][:], label_sb[1][1][:, :, cols], ALU.add)
-        nc.gpsimd.tensor_scalar(hinge_sb[1][1][:, :, 0:QUARTER], margin[1][:, pair_places(1), 0:QUARTER], CLAMP, 0.0, ALU.min, ALU.max)
+
+        last_margin = margin[1][:, pair_places(1), :]
+        for c in range(2):
+            cols = slice(c * QUARTER, (c + 1) * QUARTER)
+            nc.vector.tensor_tensor(last_margin[:, :, cols], acc_last[c][:], label_sb[1][1][:, :, cols], ALU.add)
+        hinge_on_gpsimd(hinge_sb[1][1][:, :, 0:QUARTER], last_margin[:, :, 0:QUARTER])
         nc.vector.tensor_scalar_max(*out_views(HALF, QUARTER), 0.0)
-        nc.vector.tensor_scalar_max(hinge_sb[1][1][:, :, QUARTER:HALF], margin[1][:, pair_places(1), QUARTER:HALF], 0.0)
+        nc.vector.tensor_scalar_max(hinge_sb[1][1][:, :, QUARTER:HALF], last_margin[:, :, QUARTER:HALF], 0.0)
         store_hinge(1, 1)
-        nc.scalar.activation(*out_views(J - 64, 64), RELU)
-        nc.vector.tensor_scalar_max(*out_views(HALF + QUARTER, 64), 0.0)
-        quantise_out(0, HALF)
-        nc.sync.dma_start(out_words_i32[:, half_cols(0)], out_codes[:, half_cols(0)])
-        quantise_out(HALF, HALF)
-        nc.sync.dma_start(out_words_i32[:, half_cols(1)], out_codes[:, half_cols(1)])
+        nc.scalar.activation(*out_views(J - SCALAR_TAIL, SCALAR_TAIL), RELU)
+        nc.vector.tensor_scalar_max(*out_views(HALF + QUARTER, QUARTER - SCALAR_TAIL), 0.0)
+        for v in range(2):
+            quantise_out(v)
 
         for r in range(PACK):
             queue = nc.scalar if r % 2 == 0 else nc.sync

@@ -21,6 +21,7 @@ QUADRANT = 32
 HALF = J // 2
 QUARTER = J // 4
 STAGE = P - K // 32
+SCALAR_ROUND = 64
 SCALAR_HINGE = 160
 SCALAR_TAIL = 64
 CLAMP = 3.4028234663852886e38
@@ -105,22 +106,39 @@ def tile_picked_znceg_hinge_po_kernel(tc, x_words, x_scales, hT, label, offs, ou
         out_scales = sb.tile([P, J], U8, name="out_scales", align_bytes=64)
         acc = {(t, v): psum.tile([P, HALF], F32, name=f"acc{t}{v}") for v in range(2) for t in range(PACK - 2 * v)}
         acc_last = [psum.tile([P, 2, QUARTER], F32, name=f"acc_last{c}") for c in range(2)]
-        rounded_at = (0, ROUNDED_BYTES, 2 * ROUNDED_BYTES, ROUNDED_BYTES // 2)
+        shares = (
+            ((nc.scalar.copy, 0, (QUARTER,), 0), (nc.vector.tensor_copy, QUARTER, (QUARTER,), ROUNDED_BYTES)),
+            (
+                (nc.vector.tensor_copy, 0, (QUARTER, QUARTER - SCALAR_ROUND), ROUNDED_BYTES // 4),
+                (nc.scalar.copy, HALF - SCALAR_ROUND, (SCALAR_ROUND,), 3 * ROUNDED_BYTES),
+            ),
+        )
+        h_codes = [
+            sb.tile([P, HALF], U32, name="h_codes0", align_bytes=64),
+            rounding.tile([P, HALF], U32, name="h_codes1", align_bytes=64, offset=7 * ROUNDED_BYTES // 4),
+        ]
+        h_scales = [
+            sb.tile([P, HALF], U8, name="h_scales0", align_bytes=64),
+            rounding.tile([P, HALF], U8, name="h_scales1", align_bytes=64, offset=0),
+        ]
 
         def quantise_and_multiply(v):
-            codes = sb.tile([P, HALF], U32, name=f"h_codes{v}", align_bytes=64)
-            scales = sb.tile([P, HALF], U8, name=f"h_scales{v}", align_bytes=64)
+            codes, scales = h_codes[v], h_scales[v]
             quarters = [slice(0, QUARTER), slice(QUARTER, HALF)]
-            h_bf = []
-            for c, copy in enumerate((nc.scalar.copy, nc.vector.tensor_copy)):
-                q = 2 * v + c
-                h_bf.append(rounding.tile([P, QUARTER, PACK], BF16, name=f"h_bf{q}", align_bytes=64, offset=rounded_at[q]))
-                copy(by_line(h_bf[c][:], "p (c i) t -> p c t i"), by_line(h_raw[v][:, :, quarters[c]], "p t (c i) -> p c t i"))
-            for c, cols in enumerate(quarters):
+            rounded = []
+            for copy, c0, widths, first_byte in shares[v]:
+                h_bf = rounding.tile([P, sum(widths), PACK], BF16, name=f"h_bf{v}_{c0}", align_bytes=64, offset=first_byte)
+                at = 0
+                for width in widths:
+                    cols, piece = slice(c0 + at, c0 + at + width), h_bf[:, at : at + width, :]
+                    copy(by_line(piece, "p (c i) t -> p c t i"), by_line(h_raw[v][:, :, cols], "p t (c i) -> p c t i"))
+                    rounded.append((cols, piece))
+                    at = at + width
+            for cols, piece in rounded[-v:] + rounded[: len(rounded) - v] if v else rounded:
                 nc.vector.quantize_mx(
                     out=codes[:, cols].bitcast(FP8X4),
                     scales=scales[:, cols],
-                    in_=h_bf[c][:].rearrange("p c t -> p (c t)"),
+                    in_=piece.rearrange("p c t -> p (c t)"),
                 )
             passes = [(acc[t, v][:], t, slice(0, HALF)) for t in range(PACK - 2 * v)]
             if v == 1:
@@ -181,9 +199,8 @@ def tile_picked_znceg_hinge_po_kernel(tc, x_words, x_scales, hT, label, offs, ou
         for c in range(2):
             cols = slice(c * QUARTER, (c + 1) * QUARTER)
             nc.vector.tensor_tensor(last_margin[:, :, cols], acc_last[c][:], label_sb[1][1][:, :, cols], ALU.add)
-        hinge_on_gpsimd(hinge_sb[1][1][:, :, 0:QUARTER], last_margin[:, :, 0:QUARTER])
         nc.vector.tensor_scalar_max(*out_views(HALF, QUARTER), 0.0)
-        nc.vector.tensor_scalar_max(hinge_sb[1][1][:, :, QUARTER:HALF], last_margin[:, :, QUARTER:HALF], 0.0)
+        nc.vector.tensor_scalar_max(hinge_sb[1][1][:], last_margin, 0.0)
         store_hinge(1, 1)
         nc.scalar.activation(*out_views(J - SCALAR_TAIL, SCALAR_TAIL), RELU)
         nc.vector.tensor_scalar_max(*out_views(HALF + QUARTER, QUARTER - SCALAR_TAIL), 0.0)

@@ -68,7 +68,7 @@ def tile_picked_znceg_hinge_po_kernel(tc, x_words, x_scales, hT, label, offs, ou
 
         nc.vector.memset(scale_table[0:STAGE, :].bitcast(I32), 0)
 
-        nc.sync.dma_start(scale_table[STAGE:P, :].bitcast(I32), x_scales_i32)
+        nc.scalar.dma_start(scale_table[STAGE:P, :].bitcast(I32), x_scales_i32)
         nc.sync.dma_start(offsets[:], offs)
         nc.sync.dma_start(word_table[:], x_words_i32)
         for v in range(2):

@@ -23,7 +23,7 @@ QUARTER = J // 4
 STAGE = P - K // 32
 SCALAR_ROUND = 64
 SCALAR_HINGE = 160
-SCALAR_TAIL = 64
+SCALAR_TAIL = QUARTER
 CLAMP = 3.4028234663852886e38
 
 LABEL_BYTES = 2 * HALF * 4
@@ -104,8 +104,7 @@ def tile_picked_znceg_hinge_po_kernel(tc, x_words, x_scales, hT, label, offs, ou
         hinge_sb = [[sb.tile([P, 2, HALF], F32, name=f"hinge{u}{v}", align_bytes=64) for v in range(2)] for u in range(2)]
         out_codes = sb.tile([P, J], I32, name="out_codes", align_bytes=64)
         out_scales = sb.tile([P, J], U8, name="out_scales", align_bytes=64)
-        acc = {(t, v): psum.tile([P, HALF], F32, name=f"acc{t}{v}") for v in range(2) for t in range(PACK - 2 * v)}
-        acc_last = [psum.tile([P, 2, QUARTER], F32, name=f"acc_last{c}") for c in range(2)]
+        acc = {(t, v): psum.tile([P, HALF], F32, name=f"acc{t}{v}") for v in range(2) for t in range(PACK)}
         shares = (
             ((nc.scalar.copy, 0, (QUARTER,), 0), (nc.vector.tensor_copy, QUARTER, (QUARTER,), ROUNDED_BYTES)),
             (
@@ -124,7 +123,6 @@ def tile_picked_znceg_hinge_po_kernel(tc, x_words, x_scales, hT, label, offs, ou
 
         def quantise_and_multiply(v):
             codes, scales = h_codes[v], h_scales[v]
-            quarters = [slice(0, QUARTER), slice(QUARTER, HALF)]
             rounded = []
             for copy, c0, widths, first_byte in shares[v]:
                 h_bf = rounding.tile([P, sum(widths), PACK], BF16, name=f"h_bf{v}_{c0}", align_bytes=64, offset=first_byte)
@@ -140,23 +138,26 @@ def tile_picked_znceg_hinge_po_kernel(tc, x_words, x_scales, hT, label, offs, ou
                     scales=scales[:, cols],
                     in_=piece.rearrange("p c t -> p (c t)"),
                 )
-            passes = [(acc[t, v][:], t, slice(0, HALF)) for t in range(PACK - 2 * v)]
-            if v == 1:
-                passes += [(acc_last[c][:, t - 2, :], t, quarters[c]) for c in range(2) for t in (2, 3)]
-            for out, t, cols in passes:
+            for t in range(PACK):
                 nc.tensor.matmul_mx(
-                    out=out,
+                    out=acc[t, v][:],
                     lhsT=dealt_words[:, t, :].bitcast(FP8X4),
                     lhsT_scale=dealt_scales[:, t, :],
-                    rhs=codes[:, cols].bitcast(FP8X4),
-                    rhs_scale=scales[:, cols],
+                    rhs=codes[:].bitcast(FP8X4),
+                    rhs_scale=scales[:],
                     start=True,
                     stop=True,
                 )
 
+        def add_place(t, v):
+            nc.vector.tensor_tensor(margin[v][:, t, :], acc[t, v][:], label_sb[t // 2][v][:, t % 2, :], ALU.add)
+
         def add_label(u, v):
             for t in (2 * u, 2 * u + 1):
-                nc.vector.tensor_tensor(margin[v][:, t, :], acc[t, v][:], label_sb[u][v][:, t % 2, :], ALU.add)
+                add_place(t, v)
+
+        def hinge_on_vector(t):
+            nc.vector.tensor_scalar_max(hinge_sb[t // 2][1][:, t % 2, :], margin[1][:, t, :], 0.0)
 
         def hinge_on_gpsimd(dst, src):
             nc.gpsimd.tensor_scalar(dst, src, CLAMP, 0.0, ALU.min, ALU.max)
@@ -191,19 +192,17 @@ def tile_picked_znceg_hinge_po_kernel(tc, x_words, x_scales, hT, label, offs, ou
         nc.scalar.activation(*out_views(0, QUARTER), RELU)
         add_label(0, 1)
         hinge_on_gpsimd(hinge_sb[0][1][:, 0, :], margin[1][:, 0, :])
-        nc.scalar.activation(hinge_sb[0][1][:, 1, :], margin[1][:, 1, :], RELU)
-        store_hinge(0, 1)
         nc.scalar.activation(*out_views(QUARTER, QUARTER), RELU)
 
-        last_margin = margin[1][:, pair_places(1), :]
-        for c in range(2):
-            cols = slice(c * QUARTER, (c + 1) * QUARTER)
-            nc.vector.tensor_tensor(last_margin[:, :, cols], acc_last[c][:], label_sb[1][1][:, :, cols], ALU.add)
-        nc.vector.tensor_scalar_max(*out_views(HALF, QUARTER), 0.0)
-        nc.vector.tensor_scalar_max(hinge_sb[1][1][:], last_margin, 0.0)
+        add_place(2, 1)
+        hinge_on_vector(1)
+        store_hinge(0, 1)
+        add_place(3, 1)
+        for t in (2, 3):
+            hinge_on_vector(t)
         store_hinge(1, 1)
+        nc.vector.tensor_scalar_max(*out_views(HALF, QUARTER), 0.0)
         nc.scalar.activation(*out_views(J - SCALAR_TAIL, SCALAR_TAIL), RELU)
-        nc.vector.tensor_scalar_max(*out_views(HALF + QUARTER, QUARTER - SCALAR_TAIL), 0.0)
         for v in range(2):
             quantise_out(v)
 

@@ -207,5 +207,4 @@ def tile_picked_znceg_hinge_po_kernel(tc, x_words, x_scales, hT, label, offs, ou
             quantise_out(v)
 
         for r in range(PACK):
-            queue = nc.scalar if r % 2 == 0 else nc.sync
-            queue.dma_start(out_scales_i32[r], out_scales[r:P:QUADRANT, :].bitcast(I32))
+            nc.sync.dma_start(out_scales_i32[r], out_scales[r:P:QUADRANT, :].bitcast(I32))

@@ -22,7 +22,7 @@ HALF = J // 2
 QUARTER = J // 4
 STAGE = P - K // 32
 SCALAR_ROUND = 64
-SCALAR_HINGE = 160
+SCALAR_HINGE = (160, 128)
 SCALAR_TAIL = QUARTER
 CLAMP = 3.4028234663852886e38
 
@@ -102,9 +102,11 @@ def tile_picked_znceg_hinge_po_kernel(tc, x_words, x_scales, hT, label, offs, ou
         margin = [sb.tile([P, PACK, HALF], F32, name=f"margin{v}", align_bytes=64) for v in range(2)]
         hinge_bf = [sb.tile([P, HALF, PACK], BF16, name=f"hinge_bf{v}", align_bytes=64) for v in range(2)]
         hinge_sb = [[sb.tile([P, 2, HALF], F32, name=f"hinge{u}{v}", align_bytes=64) for v in range(2)] for u in range(2)]
-        out_codes = sb.tile([P, J], I32, name="out_codes", align_bytes=64)
+        out_codes = reuse.tile([P, J], I32, name="out_codes", align_bytes=64, offset=3 * LABEL_BYTES)
         out_scales = sb.tile([P, J], U8, name="out_scales", align_bytes=64)
-        acc = {(t, v): psum.tile([P, HALF], F32, name=f"acc{t}{v}") for v in range(2) for t in range(PACK)}
+        acc = {(t, v): psum.tile([P, HALF], F32, name=f"acc{t}{v}") for v in range(2) for t in range(PACK - 2 * v)}
+        acc_last = [psum.tile([P, 2, QUARTER], F32, name=f"acc_last{c}") for c in range(2)]
+        quarters = [slice(0, QUARTER), slice(QUARTER, HALF)]
         shares = (
             ((nc.scalar.copy, 0, (QUARTER,), 0), (nc.vector.tensor_copy, QUARTER, (QUARTER,), ROUNDED_BYTES)),
             (
@@ -138,13 +140,16 @@ def tile_picked_znceg_hinge_po_kernel(tc, x_words, x_scales, hT, label, offs, ou
                     scales=scales[:, cols],
                     in_=piece.rearrange("p c t -> p (c t)"),
                 )
-            for t in range(PACK):
+            passes = [(acc[t, v][:], t, slice(0, HALF)) for t in range(PACK - 2 * v)]
+            if v == 1:
+                passes += [(acc_last[c][:, t - 2, :], t, quarters[c]) for c in range(2) for t in (2, 3)]
+            for out, t, cols in passes:
                 nc.tensor.matmul_mx(
-                    out=acc[t, v][:],
+                    out=out,
                     lhsT=dealt_words[:, t, :].bitcast(FP8X4),
                     lhsT_scale=dealt_scales[:, t, :],
-                    rhs=codes[:].bitcast(FP8X4),
-                    rhs_scale=scales[:],
+                    rhs=codes[:, cols].bitcast(FP8X4),
+                    rhs_scale=scales[:, cols],
                     start=True,
                     stop=True,
                 )
@@ -155,9 +160,6 @@ def tile_picked_znceg_hinge_po_kernel(tc, x_words, x_scales, hT, label, offs, ou
         def add_label(u, v):
             for t in (2 * u, 2 * u + 1):
                 add_place(t, v)
-
-        def hinge_on_vector(t):
-            nc.vector.tensor_scalar_max(hinge_sb[t // 2][1][:, t % 2, :], margin[1][:, t, :], 0.0)
 
         def hinge_on_gpsimd(dst, src):
             nc.gpsimd.tensor_scalar(dst, src, CLAMP, 0.0, ALU.min, ALU.max)
@@ -171,12 +173,15 @@ def tile_picked_znceg_hinge_po_kernel(tc, x_words, x_scales, hT, label, offs, ou
             src = by_line(margin[v][:, :, c : c + width], "p t (c i) -> p c t i")
             return dst, src
 
-        def quantise_out(v):
+        def quantise_out(c0, width):
+            v, c = divmod(c0, HALF)
             nc.vector.quantize_mx(
-                out=out_codes[:, half_cols(v)].bitcast(FP8X4),
-                scales=out_scales[:, half_cols(v)],
-                in_=hinge_bf[v][:].rearrange("p c t -> p (c t)"),
+                out=out_codes[:, c0 : c0 + width].bitcast(FP8X4),
+                scales=out_scales[:, c0 : c0 + width],
+                in_=hinge_bf[v][:, c : c + width, :].rearrange("p c t -> p (c t)"),
             )
+
+        def store_words(v):
             nc.sync.dma_start(out_words_i32[:, half_cols(v)], out_codes[:, half_cols(v)])
 
         for v in range(2):
@@ -186,25 +191,39 @@ def tile_picked_znceg_hinge_po_kernel(tc, x_words, x_scales, hT, label, offs, ou
             add_label(u, 0)
             dst, src = hinge_sb[u][0][:], margin[0][:, pair_places(u), :]
             nc.scalar.activation(dst[:, 0, :], src[:, 0, :], RELU)
-            nc.scalar.activation(dst[:, 1, 0:SCALAR_HINGE], src[:, 1, 0:SCALAR_HINGE], RELU)
-            hinge_on_gpsimd(dst[:, 1, SCALAR_HINGE:HALF], src[:, 1, SCALAR_HINGE:HALF])
-            store_hinge(u, 0)
+            split = SCALAR_HINGE[u]
+            nc.scalar.activation(dst[:, 1, 0:split], src[:, 1, 0:split], RELU)
+            hinge_on_gpsimd(dst[:, 1, split:HALF], src[:, 1, split:HALF])
+            if u == 0:
+                for t in range(2):
+                    nc.sync.dma_start(out_rows[:, t, half_cols(0)], dst[:, t, :])
+            else:
+                store_hinge(u, 0)
         nc.scalar.activation(*out_views(0, QUARTER), RELU)
         add_label(0, 1)
         hinge_on_gpsimd(hinge_sb[0][1][:, 0, :], margin[1][:, 0, :])
         nc.scalar.activation(*out_views(QUARTER, QUARTER), RELU)
 
-        add_place(2, 1)
-        hinge_on_vector(1)
+        last_margin = [margin[1][:, pair_places(1), cols] for cols in quarters]
+        last_hinge = [hinge_sb[1][1][:, :, cols] for cols in quarters]
+
+        def add_last(c):
+            nc.vector.tensor_tensor(last_margin[c], acc_last[c][:], label_sb[1][1][:, :, quarters[c]], ALU.add)
+
+        add_last(0)
+        nc.vector.tensor_scalar_max(hinge_sb[0][1][:, 1, :], margin[1][:, 1, :], 0.0)
         store_hinge(0, 1)
-        add_place(3, 1)
-        for t in (2, 3):
-            hinge_on_vector(t)
+        add_last(1)
+        for c in range(2):
+            nc.vector.tensor_scalar_max(last_hinge[c], last_margin[c], 0.0)
+            nc.vector.tensor_scalar_max(*out_views(HALF + c * (QUARTER // 2), QUARTER // 2), 0.0)
         store_hinge(1, 1)
-        nc.vector.tensor_scalar_max(*out_views(HALF, QUARTER), 0.0)
         nc.scalar.activation(*out_views(J - SCALAR_TAIL, SCALAR_TAIL), RELU)
-        for v in range(2):
-            quantise_out(v)
+        quantise_out(0, HALF)
+        store_words(0)
+        for c0 in (HALF, HALF + QUARTER):
+            quantise_out(c0, QUARTER)
+        store_words(1)
 
         for r in range(PACK):
             nc.sync.dma_start(out_scales_i32[r], out_scales[r:P:QUADRANT, :].bitcast(I32))

@@ -26,7 +26,7 @@ SCALAR_HINGE = (160, 128)
 SCALAR_TAIL = QUARTER
 CLAMP = 3.4028234663852886e38
 
-LABEL_BYTES = 2 * HALF * 4
+PLACE_BYTES = HALF * 4
 ROUNDED_BYTES = QUARTER * PACK * 2
 
 
@@ -58,8 +58,8 @@ def tile_picked_znceg_hinge_po_kernel(tc, x_words, x_scales, hT, label, offs, ou
         reuse = ctx.enter_context(tc.tile_pool(name="reuse", bufs=1))
         psum = ctx.enter_context(tc.psum_pool(name="psum", bufs=1))
 
-        word_table_at = 2 * LABEL_BYTES
-        picked_at = (word_table_at + 4 * T, LABEL_BYTES - S // 4)
+        word_table_at = 5 * PLACE_BYTES
+        picked_at = (word_table_at + 4 * T, 3 * PLACE_BYTES - S // 4)
 
         offsets = sb.tile([P, S // 16], U16, name="offsets")
         word_table = reuse.tile([P, T], I32, name="word_table", offset=word_table_at)
@@ -89,22 +89,24 @@ def tile_picked_znceg_hinge_po_kernel(tc, x_words, x_scales, hT, label, offs, ou
         for r in range(PACK):
             nc.sync.dma_start(dealt_rows[r:STAGE:QUADRANT, :].bitcast(I32), dealt_rows[STAGE + r : P : PACK, :].bitcast(I32))
 
-        label_sb = [
-            [reuse.tile([P, 2, HALF], F32, name=f"label{u}{v}", offset=LABEL_BYTES * (2 * v + u)) for v in range(2)]
-            for u in range(2)
-        ]
-        for u in range(2):
-            nc.sync.dma_start(label_sb[u][0][:], label_rows[:, pair_places(u), half_cols(0)])
+        label_lower = reuse.tile([P, 3, HALF], F32, name="label_lower", offset=0)
+        label_last_place = reuse.tile([P, J], F32, name="label_last_place", offset=3 * PLACE_BYTES)
+        label_upper = reuse.tile([P, 3, HALF], F32, name="label_upper", offset=word_table_at)
+        nc.sync.dma_start(label_lower[:], label_rows[:, 0:3, half_cols(0)])
+        nc.sync.dma_start(label_last_place[:], label_rows[:, 3, :])
         nc.vector.tensor_copy(dealt_words[:].rearrange("p t m -> p m t"), word_table[:].bitcast(U32).indirect(offsets[:]))
-        for u in range(2):
-            nc.sync.dma_start(label_sb[u][1][:], label_rows[:, pair_places(u), half_cols(1)])
+        nc.sync.dma_start(label_upper[:], label_rows[:, 0:3, half_cols(1)])
+
+        def label_of(t, v):
+            return label_last_place[:, half_cols(v)] if t == 3 else (label_lower, label_upper)[v][:, t, :]
 
         margin = [sb.tile([P, PACK, HALF], F32, name=f"margin{v}", align_bytes=64) for v in range(2)]
         hinge_bf = [sb.tile([P, HALF, PACK], BF16, name=f"hinge_bf{v}", align_bytes=64) for v in range(2)]
         hinge_sb = [[sb.tile([P, 2, HALF], F32, name=f"hinge{u}{v}", align_bytes=64) for v in range(2)] for u in range(2)]
-        out_codes = reuse.tile([P, J], I32, name="out_codes", align_bytes=64, offset=3 * LABEL_BYTES)
+        out_codes = reuse.tile([P, J], I32, name="out_codes", align_bytes=64, offset=word_table_at)
         out_scales = sb.tile([P, J], U8, name="out_scales", align_bytes=64)
-        acc = {(t, v): psum.tile([P, HALF], F32, name=f"acc{t}{v}") for v in range(2) for t in range(PACK - 2 * v)}
+        whole_places = ((0, 1, 2, 3), (3, 0))
+        acc = {(t, v): psum.tile([P, HALF], F32, name=f"acc{t}{v}") for v in range(2) for t in whole_places[v]}
         acc_last = [psum.tile([P, 2, QUARTER], F32, name=f"acc_last{c}") for c in range(2)]
         quarters = [slice(0, QUARTER), slice(QUARTER, HALF)]
         shares = (
@@ -140,9 +142,9 @@ def tile_picked_znceg_hinge_po_kernel(tc, x_words, x_scales, hT, label, offs, ou
                     scales=scales[:, cols],
                     in_=piece.rearrange("p c t -> p (c t)"),
                 )
-            passes = [(acc[t, v][:], t, slice(0, HALF)) for t in range(PACK - 2 * v)]
+            passes = [(acc[t, v][:], t, slice(0, HALF)) for t in whole_places[v]]
             if v == 1:
-                passes += [(acc_last[c][:, t - 2, :], t, quarters[c]) for c in range(2) for t in (2, 3)]
+                passes += [(acc_last[c][:, t - 1, :], t, quarters[c]) for c in range(2) for t in (1, 2)]
             for out, t, cols in passes:
                 nc.tensor.matmul_mx(
                     out=out,
@@ -155,7 +157,7 @@ def tile_picked_znceg_hinge_po_kernel(tc, x_words, x_scales, hT, label, offs, ou
                 )
 
         def add_place(t, v):
-            nc.vector.tensor_tensor(margin[v][:, t, :], acc[t, v][:], label_sb[t // 2][v][:, t % 2, :], ALU.add)
+            nc.vector.tensor_tensor(margin[v][:, t, :], acc[t, v][:], label_of(t, v), ALU.add)
 
         def add_label(u, v):
             for t in (2 * u, 2 * u + 1):
@@ -165,7 +167,8 @@ def tile_picked_znceg_hinge_po_kernel(tc, x_words, x_scales, hT, label, offs, ou
             nc.gpsimd.tensor_scalar(dst, src, CLAMP, 0.0, ALU.min, ALU.max)
 
         def store_hinge(u, v):
-            nc.sync.dma_start(out_rows[:, pair_places(u), half_cols(v)], hinge_sb[u][v][:])
+            places = (pair_places(u), (slice(0, 4, 3), slice(1, 3))[u])[v]
+            nc.sync.dma_start(out_rows[:, places, half_cols(v)], hinge_sb[u][v][:])
 
         def out_views(c0, width):
             v, c = divmod(c0, HALF)
@@ -200,18 +203,19 @@ def tile_picked_znceg_hinge_po_kernel(tc, x_words, x_scales, hT, label, offs, ou
             else:
                 store_hinge(u, 0)
         nc.scalar.activation(*out_views(0, QUARTER), RELU)
-        add_label(0, 1)
-        hinge_on_gpsimd(hinge_sb[0][1][:, 0, :], margin[1][:, 0, :])
+        add_place(3, 1)
+        add_place(0, 1)
+        hinge_on_gpsimd(hinge_sb[0][1][:, 1, :], margin[1][:, 3, :])
         nc.scalar.activation(*out_views(QUARTER, QUARTER), RELU)
 
-        last_margin = [margin[1][:, pair_places(1), cols] for cols in quarters]
+        last_margin = [margin[1][:, 1:3, cols] for cols in quarters]
         last_hinge = [hinge_sb[1][1][:, :, cols] for cols in quarters]
 
         def add_last(c):
-            nc.vector.tensor_tensor(last_margin[c], acc_last[c][:], label_sb[1][1][:, :, quarters[c]], ALU.add)
+            nc.vector.tensor_tensor(last_margin[c], acc_last[c][:], label_upper[:, 1:3, quarters[c]], ALU.add)
 
         add_last(0)
-        nc.vector.tensor_scalar_max(hinge_sb[0][1][:, 1, :], margin[1][:, 1, :], 0.0)
+        nc.vector.tensor_scalar_max(hinge_sb[0][1][:, 0, :], margin[1][:, 0, :], 0.0)
         store_hinge(0, 1)
         add_last(1)
         for c in range(2):

@@ -23,7 +23,7 @@ QUARTER = J // 4
 STAGE = P - K // 32
 SCALAR_ROUND = 64
 SCALAR_HINGE = (160, 128)
-SCALAR_TAIL = QUARTER
+SCALAR_TAIL = QUARTER // 2
 CLAMP = 3.4028234663852886e38
 
 PLACE_BYTES = HALF * 4
@@ -58,7 +58,7 @@ def tile_picked_znceg_hinge_po_kernel(tc, x_words, x_scales, hT, label, offs, ou
         reuse = ctx.enter_context(tc.tile_pool(name="reuse", bufs=1))
         psum = ctx.enter_context(tc.psum_pool(name="psum", bufs=1))
 
-        word_table_at = 5 * PLACE_BYTES
+        word_table_at = 6 * PLACE_BYTES
         picked_at = (word_table_at + 4 * T, 3 * PLACE_BYTES - S // 4)
 
         offsets = sb.tile([P, S // 16], U16, name="offsets")
@@ -89,23 +89,35 @@ def tile_picked_znceg_hinge_po_kernel(tc, x_words, x_scales, hT, label, offs, ou
         for r in range(PACK):
             nc.sync.dma_start(dealt_rows[r:STAGE:QUADRANT, :].bitcast(I32), dealt_rows[STAGE + r : P : PACK, :].bitcast(I32))
 
-        label_lower = reuse.tile([P, 3, HALF], F32, name="label_lower", offset=0)
-        label_last_place = reuse.tile([P, J], F32, name="label_last_place", offset=3 * PLACE_BYTES)
-        label_upper = reuse.tile([P, 3, HALF], F32, name="label_upper", offset=word_table_at)
-        nc.sync.dma_start(label_lower[:], label_rows[:, 0:3, half_cols(0)])
-        nc.sync.dma_start(label_last_place[:], label_rows[:, 3, :])
+        label_first = reuse.tile([P, 3, HALF], F32, name="label_first", offset=0)
+        label_second = reuse.tile([P, 3, HALF], F32, name="label_second", offset=3 * PLACE_BYTES)
+        label_third = reuse.tile([P, 2, HALF], F32, name="label_third", offset=word_table_at)
+        label_halves = label.rearrange("(p t) (v c) -> p (t v) c", t=PACK, v=2)
+        nc.sync.dma_start(label_first[:], label_rows[:, 0:3, half_cols(0)])
+        nc.sync.dma_start(label_second[:], label_halves[:, 5:8, :])
         nc.vector.tensor_copy(dealt_words[:].rearrange("p t m -> p m t"), word_table[:].bitcast(U32).indirect(offsets[:]))
-        nc.sync.dma_start(label_upper[:], label_rows[:, 0:3, half_cols(1)])
+        nc.sync.dma_start(label_third[:], label_rows[:, 0:2, half_cols(1)])
 
         def label_of(t, v):
-            return label_last_place[:, half_cols(v)] if t == 3 else (label_lower, label_upper)[v][:, t, :]
+            if 2 * t + v >= 5:
+                return label_second[:, 2 * t + v - 5, :]
+            return (label_first, label_third)[v][:, t, :]
 
         margin = [sb.tile([P, PACK, HALF], F32, name=f"margin{v}", align_bytes=64) for v in range(2)]
-        hinge_bf = [sb.tile([P, HALF, PACK], BF16, name=f"hinge_bf{v}", align_bytes=64) for v in range(2)]
+        hinge_bf = {
+            0: sb.tile([P, QUARTER, PACK], BF16, name="hinge_bf0", align_bytes=64),
+            QUARTER: reuse.tile([P, QUARTER, PACK], BF16, name="hinge_bf1", align_bytes=64, offset=4 * PLACE_BYTES),
+            HALF: sb.tile([P, HALF, PACK], BF16, name="hinge_bf2", align_bytes=64),
+        }
+
+        def rounded_out(c0, width):
+            first = max(c for c in hinge_bf if c <= c0)
+            return hinge_bf[first][:, c0 - first : c0 - first + width, :]
+
         hinge_sb = [[sb.tile([P, 2, HALF], F32, name=f"hinge{u}{v}", align_bytes=64) for v in range(2)] for u in range(2)]
         out_codes = reuse.tile([P, J], I32, name="out_codes", align_bytes=64, offset=word_table_at)
         out_scales = sb.tile([P, J], U8, name="out_scales", align_bytes=64)
-        whole_places = ((0, 1, 2, 3), (3, 0))
+        whole_places = ((0, 1, 2, 3), (3, 2))
         acc = {(t, v): psum.tile([P, HALF], F32, name=f"acc{t}{v}") for v in range(2) for t in whole_places[v]}
         acc_last = [psum.tile([P, 2, QUARTER], F32, name=f"acc_last{c}") for c in range(2)]
         quarters = [slice(0, QUARTER), slice(QUARTER, HALF)]
@@ -144,7 +156,7 @@ def tile_picked_znceg_hinge_po_kernel(tc, x_words, x_scales, hT, label, offs, ou
                 )
             passes = [(acc[t, v][:], t, slice(0, HALF)) for t in whole_places[v]]
             if v == 1:
-                passes += [(acc_last[c][:, t - 1, :], t, quarters[c]) for c in range(2) for t in (1, 2)]
+                passes += [(acc_last[c][:, t, :], t, quarters[c]) for c in range(2) for t in (0, 1)]
             for out, t, cols in passes:
                 nc.tensor.matmul_mx(
                     out=out,
@@ -167,21 +179,19 @@ def tile_picked_znceg_hinge_po_kernel(tc, x_words, x_scales, hT, label, offs, ou
             nc.gpsimd.tensor_scalar(dst, src, CLAMP, 0.0, ALU.min, ALU.max)
 
         def store_hinge(u, v):
-            places = (pair_places(u), (slice(0, 4, 3), slice(1, 3))[u])[v]
-            nc.sync.dma_start(out_rows[:, places, half_cols(v)], hinge_sb[u][v][:])
+            nc.sync.dma_start(out_rows[:, pair_places(u), half_cols(v)], hinge_sb[u][v][:])
 
         def out_views(c0, width):
             v, c = divmod(c0, HALF)
-            dst = by_line(hinge_bf[v][:, c : c + width, :], "p (c i) t -> p c t i")
+            dst = by_line(rounded_out(c0, width), "p (c i) t -> p c t i")
             src = by_line(margin[v][:, :, c : c + width], "p t (c i) -> p c t i")
             return dst, src
 
         def quantise_out(c0, width):
-            v, c = divmod(c0, HALF)
             nc.vector.quantize_mx(
                 out=out_codes[:, c0 : c0 + width].bitcast(FP8X4),
                 scales=out_scales[:, c0 : c0 + width],
-                in_=hinge_bf[v][:, c : c + width, :].rearrange("p c t -> p (c t)"),
+                in_=rounded_out(c0, width).rearrange("p c t -> p (c t)"),
             )
 
         def store_words(v):
@@ -204,26 +214,28 @@ def tile_picked_znceg_hinge_po_kernel(tc, x_words, x_scales, hT, label, offs, ou
                 store_hinge(u, 0)
         nc.scalar.activation(*out_views(0, QUARTER), RELU)
         add_place(3, 1)
-        add_place(0, 1)
-        hinge_on_gpsimd(hinge_sb[0][1][:, 1, :], margin[1][:, 3, :])
+        add_place(2, 1)
+        hinge_on_gpsimd(hinge_sb[1][1][:, 1, :], margin[1][:, 3, :])
+        nc.scalar.activation(hinge_sb[1][1][:, 0, :], margin[1][:, 2, :], RELU)
+        store_hinge(1, 1)
         nc.scalar.activation(*out_views(QUARTER, QUARTER), RELU)
 
-        last_margin = [margin[1][:, 1:3, cols] for cols in quarters]
-        last_hinge = [hinge_sb[1][1][:, :, cols] for cols in quarters]
+        last_margin = [margin[1][:, 0:2, cols] for cols in quarters]
+        last_hinge = [hinge_sb[0][1][:, :, cols] for cols in quarters]
 
         def add_last(c):
-            nc.vector.tensor_tensor(last_margin[c], acc_last[c][:], label_upper[:, 1:3, quarters[c]], ALU.add)
+            nc.vector.tensor_tensor(last_margin[c], acc_last[c][:], label_third[:, :, quarters[c]], ALU.add)
 
         add_last(0)
-        nc.vector.tensor_scalar_max(hinge_sb[0][1][:, 0, :], margin[1][:, 0, :], 0.0)
-        store_hinge(0, 1)
         add_last(1)
         for c in range(2):
             nc.vector.tensor_scalar_max(last_hinge[c], last_margin[c], 0.0)
             nc.vector.tensor_scalar_max(*out_views(HALF + c * (QUARTER // 2), QUARTER // 2), 0.0)
-        store_hinge(1, 1)
+        store_hinge(0, 1)
+        nc.vector.tensor_scalar_max(*out_views(HALF + QUARTER, QUARTER - SCALAR_TAIL), 0.0)
         nc.scalar.activation(*out_views(J - SCALAR_TAIL, SCALAR_TAIL), RELU)
-        quantise_out(0, HALF)
+        for c0 in (0, QUARTER):
+            quantise_out(c0, QUARTER)
         store_words(0)
         for c0 in (HALF, HALF + QUARTER):
             quantise_out(c0, QUARTER)

@@ -22,8 +22,8 @@ HALF = J // 2
 QUARTER = J // 4
 STAGE = P - K // 32
 SCALAR_ROUND = 64
-SCALAR_HINGE = (160, 128)
-SCALAR_TAIL = QUARTER // 2
+SCALAR_HINGE = (160, HALF)
+SCALAR_TAIL = 112
 CLAMP = 3.4028234663852886e38
 
 PLACE_BYTES = HALF * 4
@@ -106,16 +106,25 @@ def tile_picked_znceg_hinge_po_kernel(tc, x_words, x_scales, hT, label, offs, ou
         margin = [sb.tile([P, PACK, HALF], F32, name=f"margin{v}", align_bytes=64) for v in range(2)]
         hinge_bf = {
             0: sb.tile([P, QUARTER, PACK], BF16, name="hinge_bf0", align_bytes=64),
-            QUARTER: reuse.tile([P, QUARTER, PACK], BF16, name="hinge_bf1", align_bytes=64, offset=4 * PLACE_BYTES),
-            HALF: sb.tile([P, HALF, PACK], BF16, name="hinge_bf2", align_bytes=64),
+            QUARTER: reuse.tile([P, QUARTER, PACK], BF16, name="hinge_bf1", align_bytes=64, offset=3 * PLACE_BYTES),
+            HALF: reuse.tile([P, HALF, PACK], BF16, name="hinge_bf2", align_bytes=64, offset=word_table_at + 2 * PLACE_BYTES - 64),
         }
 
         def rounded_out(c0, width):
             first = max(c for c in hinge_bf if c <= c0)
             return hinge_bf[first][:, c0 - first : c0 - first + width, :]
 
-        hinge_sb = [[sb.tile([P, 2, HALF], F32, name=f"hinge{u}{v}", align_bytes=64) for v in range(2)] for u in range(2)]
-        out_codes = reuse.tile([P, J], I32, name="out_codes", align_bytes=64, offset=word_table_at)
+        hinge_sb = [
+            [
+                sb.tile([P, 2, HALF], F32, name="hinge00", align_bytes=64),
+                reuse.tile([P, 2, HALF], F32, name="hinge01", align_bytes=64, offset=word_table_at - 2 * PLACE_BYTES + 64),
+            ],
+            [sb.tile([P, 2, HALF], F32, name=f"hinge1{v}", align_bytes=64) for v in range(2)],
+        ]
+        out_codes = [
+            reuse.tile([P, HALF], I32, name="out_codes0", align_bytes=64, offset=word_table_at + 64),
+            sb.tile([P, HALF], I32, name="out_codes1", align_bytes=64),
+        ]
         out_scales = sb.tile([P, J], U8, name="out_scales", align_bytes=64)
         whole_places = ((0, 1, 2, 3), (3, 2))
         acc = {(t, v): psum.tile([P, HALF], F32, name=f"acc{t}{v}") for v in range(2) for t in whole_places[v]}
@@ -189,13 +198,13 @@ def tile_picked_znceg_hinge_po_kernel(tc, x_words, x_scales, hT, label, offs, ou
 
         def quantise_out(c0, width):
             nc.vector.quantize_mx(
-                out=out_codes[:, c0 : c0 + width].bitcast(FP8X4),
+                out=out_codes[c0 // HALF][:, c0 % HALF : c0 % HALF + width].bitcast(FP8X4),
                 scales=out_scales[:, c0 : c0 + width],
                 in_=rounded_out(c0, width).rearrange("p c t -> p (c t)"),
             )
 
         def store_words(v):
-            nc.sync.dma_start(out_words_i32[:, half_cols(v)], out_codes[:, half_cols(v)])
+            nc.sync.dma_start(out_words_i32[:, half_cols(v)], out_codes[v][:])
 
         for v in range(2):
             quantise_and_multiply(v)
@@ -206,16 +215,17 @@ def tile_picked_znceg_hinge_po_kernel(tc, x_words, x_scales, hT, label, offs, ou
             nc.scalar.activation(dst[:, 0, :], src[:, 0, :], RELU)
             split = SCALAR_HINGE[u]
             nc.scalar.activation(dst[:, 1, 0:split], src[:, 1, 0:split], RELU)
-            hinge_on_gpsimd(dst[:, 1, split:HALF], src[:, 1, split:HALF])
+            if split < HALF:
+                hinge_on_gpsimd(dst[:, 1, split:HALF], src[:, 1, split:HALF])
             if u == 0:
                 for t in range(2):
                     nc.sync.dma_start(out_rows[:, t, half_cols(0)], dst[:, t, :])
             else:
                 store_hinge(u, 0)
-        nc.scalar.activation(*out_views(0, QUARTER), RELU)
+        hinge_on_gpsimd(rounded_out(0, QUARTER), margin[0][:, :, quarters[0]].rearrange("p t c -> p c t"))
         add_place(3, 1)
+        nc.scalar.activation(hinge_sb[1][1][:, 1, :], margin[1][:, 3, :], RELU)
         add_place(2, 1)
-        hinge_on_gpsimd(hinge_sb[1][1][:, 1, :], margin[1][:, 3, :])
         nc.scalar.activation(hinge_sb[1][1][:, 0, :], margin[1][:, 2, :], RELU)
         store_hinge(1, 1)
         nc.scalar.activation(*out_views(QUARTER, QUARTER), RELU)
@@ -226,13 +236,13 @@ def tile_picked_znceg_hinge_po_kernel(tc, x_words, x_scales, hT, label, offs, ou
         def add_last(c):
             nc.vector.tensor_tensor(last_margin[c], acc_last[c][:], label_third[:, :, quarters[c]], ALU.add)
 
+        vector_round = (HALF - SCALAR_TAIL) // 2
         add_last(0)
         add_last(1)
         for c in range(2):
             nc.vector.tensor_scalar_max(last_hinge[c], last_margin[c], 0.0)
-            nc.vector.tensor_scalar_max(*out_views(HALF + c * (QUARTER // 2), QUARTER // 2), 0.0)
+            nc.vector.tensor_scalar_max(*out_views(HALF + c * vector_round, vector_round), 0.0)
         store_hinge(0, 1)
-        nc.vector.tensor_scalar_max(*out_views(HALF + QUARTER, QUARTER - SCALAR_TAIL), 0.0)
         nc.scalar.activation(*out_views(J - SCALAR_TAIL, SCALAR_TAIL), RELU)
         for c0 in (0, QUARTER):
             quantise_out(c0, QUARTER)

from contextlib import ExitStack

import concourse.mybir as mybir

K, T, S, J = 512, 2048, 512, 512
FLOPS = 2 * K * S * J

F32 = mybir.dt.float32
BF16 = mybir.dt.bfloat16
I32 = mybir.dt.int32
U32 = mybir.dt.uint32
U16 = mybir.dt.uint16
U8 = mybir.dt.uint8
FP8X4 = mybir.dt.float8_e4m3fn_x4
ALU = mybir.AluOpType
RELU = mybir.ActivationFunctionType.Relu

P = 128
PACK = 4
QUADRANT = 32
HALF = J // 2
QUARTER = J // 4
STAGE = P - K // 32
SCALAR_ROUND = 64
SCALAR_HINGE = (160, HALF)
SCALAR_TAIL = 112
CLAMP = 3.4028234663852886e38

PLACE_BYTES = HALF * 4
ROUNDED_BYTES = QUARTER * PACK * 2


def by_line(ap, text):
    return ap.rearrange(text, i=4)


def half_cols(v):
    return slice(v * HALF, (v + 1) * HALF)


def pair_places(u):
    return slice(2 * u, 2 * u + 2)


def tile_picked_znceg_hinge_po_kernel(tc, x_words, x_scales, hT, label, offs, out_0, out_1, out_2):
    nc = tc.nc
    h_rows = hT.rearrange("(p t) j -> p t j", t=PACK)
    label_rows = label.rearrange("(p t) j -> p t j", t=PACK)
    out_rows = out_0.rearrange("(p t) j -> p t j", t=PACK)
    x_words_i32 = x_words[0].rearrange("p c t -> p (c t)").bitcast(I32)
    x_scales_i32 = x_scales[0].bitcast(I32)
    out_words_i32 = out_1[0].rearrange("p c t -> p (c t)").bitcast(I32)
    out_scales_i32 = out_2[0].bitcast(I32).rearrange("(q r) c -> r q c", r=PACK)

    with ExitStack() as ctx:
        sb = ctx.enter_context(tc.tile_pool(name="sb", bufs=1))
        rounding = ctx.enter_context(tc.tile_pool(name="rounding", bufs=1))
        reuse = ctx.enter_context(tc.tile_pool(name="reuse", bufs=1))
        psum = ctx.enter_context(tc.psum_pool(name="psum", bufs=1))

        word_table_at = 6 * PLACE_BYTES
        picked_at = (word_table_at + 4 * T, 3 * PLACE_BYTES - S // 4)

        offsets = sb.tile([P, S // 16], U16, name="offsets")
        word_table = reuse.tile([P, T], I32, name="word_table", offset=word_table_at)
        scale_table = sb.tile([P, T], U8, name="scale_table", align_bytes=64)
        h_raw = [sb.tile([P, PACK, HALF], F32, name=f"h_raw{v}", align_bytes=64) for v in range(2)]

        nc.vector.memset(scale_table[0:STAGE, :].bitcast(I32), 0)

        nc.scalar.dma_start(scale_table[STAGE:P, :].bitcast(I32), x_scales_i32)
        nc.sync.dma_start(offsets[:], offs)
        nc.sync.dma_start(word_table[:], x_words_i32)
        for v in range(2):
            nc.sync.dma_start(h_raw[v][:], h_rows[:, :, half_cols(v)])

        picked_scales = [reuse.tile([P, S // 2], U8, name=f"picked_scales{g}", offset=picked_at[g]) for g in range(2)]
        dealt_scales = sb.tile([P, PACK, P], U8, name="dealt_scales", align_bytes=64)
        dealt_words = sb.tile([P, PACK, P], U32, name="dealt_words", align_bytes=64)
        for g in range(2):
            entries = offsets[:, g * (S // 32) : (g + 1) * (S // 32)]
            nc.vector.tensor_copy(picked_scales[g][:], scale_table[:].indirect(entries))
        for g in range(2):
            nc.vector.tensor_copy(
                dealt_scales[:, :, g * (P // 2) : (g + 1) * (P // 2)],
                picked_scales[g][:].rearrange("p (m t) -> p t m", t=PACK),
            )
        dealt_rows = dealt_scales[:].rearrange("p t m -> p (t m)")
        for r in range(PACK):
            nc.sync.dma_start(dealt_rows[r:STAGE:QUADRANT, :].bitcast(I32), dealt_rows[STAGE + r : P : PACK, :].bitcast(I32))

        label_first = reuse.tile([P, 3, HALF], F32, name="label_first", offset=0)
        label_second = reuse.tile([P, 3, HALF], F32, name="label_second", offset=3 * PLACE_BYTES)
        label_third = reuse.tile([P, 2, HALF], F32, name="label_third", offset=word_table_at)
        label_halves = label.rearrange("(p t) (v c) -> p (t v) c", t=PACK, v=2)
        nc.sync.dma_start(label_first[:], label_rows[:, 0:3, half_cols(0)])
        nc.sync.dma_start(label_second[:], label_halves[:, 5:8, :])
        nc.vector.tensor_copy(dealt_words[:].rearrange("p t m -> p m t"), word_table[:].bitcast(U32).indirect(offsets[:]))
        nc.sync.dma_start(label_third[:], label_rows[:, 0:2, half_cols(1)])

        def label_of(t, v):
            if 2 * t + v >= 5:
                return label_second[:, 2 * t + v - 5, :]
            return (label_first, label_third)[v][:, t, :]

        margin = [sb.tile([P, PACK, HALF], F32, name=f"margin{v}", align_bytes=64) for v in range(2)]
        hinge_bf = {
            0: sb.tile([P, QUARTER, PACK], BF16, name="hinge_bf0", align_bytes=64),
            QUARTER: reuse.tile([P, QUARTER, PACK], BF16, name="hinge_bf1", align_bytes=64, offset=3 * PLACE_BYTES),
            HALF: reuse.tile([P, HALF, PACK], BF16, name="hinge_bf2", align_bytes=64, offset=word_table_at + 2 * PLACE_BYTES - 64),
        }

        def rounded_out(c0, width):
            first = max(c for c in hinge_bf if c <= c0)
            return hinge_bf[first][:, c0 - first : c0 - first + width, :]

        hinge_sb = [
            [
                sb.tile([P, 2, HALF], F32, name="hinge00", align_bytes=64),
                reuse.tile([P, 2, HALF], F32, name="hinge01", align_bytes=64, offset=word_table_at - 2 * PLACE_BYTES + 64),
            ],
            [sb.tile([P, 2, HALF], F32, name=f"hinge1{v}", align_bytes=64) for v in range(2)],
        ]
        out_codes = [
            reuse.tile([P, HALF], I32, name="out_codes0", align_bytes=64, offset=word_table_at + 64),
            sb.tile([P, HALF], I32, name="out_codes1", align_bytes=64),
        ]
        out_scales = sb.tile([P, J], U8, name="out_scales", align_bytes=64)
        whole_places = ((0, 1, 2, 3), (3, 2))
        acc = {(t, v): psum.tile([P, HALF], F32, name=f"acc{t}{v}") for v in range(2) for t in whole_places[v]}
        acc_last = [psum.tile([P, 2, QUARTER], F32, name=f"acc_last{c}") for c in range(2)]
        quarters = [slice(0, QUARTER), slice(QUARTER, HALF)]
        shares = (
            ((nc.scalar.copy, 0, (QUARTER,), 0), (nc.vector.tensor_copy, QUARTER, (QUARTER,), ROUNDED_BYTES)),
            (
                (nc.vector.tensor_copy, 0, (QUARTER, QUARTER - SCALAR_ROUND), ROUNDED_BYTES // 4),
                (nc.scalar.copy, HALF - SCALAR_ROUND, (SCALAR_ROUND,), 3 * ROUNDED_BYTES),
            ),
        )
        h_codes = [
            sb.tile([P, HALF], U32, name="h_codes0", align_bytes=64),
            rounding.tile([P, HALF], U32, name="h_codes1", align_bytes=64, offset=7 * ROUNDED_BYTES // 4),
        ]
        h_scales = [
            sb.tile([P, HALF], U8, name="h_scales0", align_bytes=64),
            rounding.tile([P, HALF], U8, name="h_scales1", align_bytes=64, offset=0),
        ]

        def quantise_and_multiply(v):
            codes, scales = h_codes[v], h_scales[v]
            rounded = []
            for copy, c0, widths, first_byte in shares[v]:
                h_bf = rounding.tile([P, sum(widths), PACK], BF16, name=f"h_bf{v}_{c0}", align_bytes=64, offset=first_byte)
                at = 0
                for width in widths:
                    cols, piece = slice(c0 + at, c0 + at + width), h_bf[:, at : at + width, :]
                    copy(by_line(piece, "p (c i) t -> p c t i"), by_line(h_raw[v][:, :, cols], "p t (c i) -> p c t i"))
                    rounded.append((cols, piece))
                    at = at + width
            for cols, piece in rounded[-v:] + rounded[: len(rounded) - v] if v else rounded:
                nc.vector.quantize_mx(
                    out=codes[:, cols].bitcast(FP8X4),
                    scales=scales[:, cols],
                    in_=piece.rearrange("p c t -> p (c t)"),
                )
            passes = [(acc[t, v][:], t, slice(0, HALF)) for t in whole_places[v]]
            if v == 1:
                passes += [(acc_last[c][:, t, :], t, quarters[c]) for c in range(2) for t in (0, 1)]
            for out, t, cols in passes:
                nc.tensor.matmul_mx(
                    out=out,
                    lhsT=dealt_words[:, t, :].bitcast(FP8X4),
                    lhsT_scale=dealt_scales[:, t, :],
                    rhs=codes[:, cols].bitcast(FP8X4),
                    rhs_scale=scales[:, cols],
                    start=True,
                    stop=True,
                )

        def add_place(t, v):
            nc.vector.tensor_tensor(margin[v][:, t, :], acc[t, v][:], label_of(t, v), ALU.add)

        def add_label(u, v):
            for t in (2 * u, 2 * u + 1):
                add_place(t, v)

        def hinge_on_gpsimd(dst, src):
            nc.gpsimd.tensor_scalar(dst, src, CLAMP, 0.0, ALU.min, ALU.max)

        def store_hinge(u, v):
            nc.sync.dma_start(out_rows[:, pair_places(u), half_cols(v)], hinge_sb[u][v][:])

        def out_views(c0, width):
            v, c = divmod(c0, HALF)
            dst = by_line(rounded_out(c0, width), "p (c i) t -> p c t i")
            src = by_line(margin[v][:, :, c : c + width], "p t (c i) -> p c t i")
            return dst, src

        def quantise_out(c0, width):
            nc.vector.quantize_mx(
                out=out_codes[c0 // HALF][:, c0 % HALF : c0 % HALF + width].bitcast(FP8X4),
                scales=out_scales[:, c0 : c0 + width],
                in_=rounded_out(c0, width).rearrange("p c t -> p (c t)"),
            )

        def store_words(v):
            nc.sync.dma_start(out_words_i32[:, half_cols(v)], out_codes[v][:])

        for v in range(2):
            quantise_and_multiply(v)

        for u in range(2):
            add_label(u, 0)
            dst, src = hinge_sb[u][0][:], margin[0][:, pair_places(u), :]
            nc.scalar.activation(dst[:, 0, :], src[:, 0, :], RELU)
            split = SCALAR_HINGE[u]
            nc.scalar.activation(dst[:, 1, 0:split], src[:, 1, 0:split], RELU)
            if split < HALF:
                hinge_on_gpsimd(dst[:, 1, split:HALF], src[:, 1, split:HALF])
            if u == 0:
                for t in range(2):
                    nc.sync.dma_start(out_rows[:, t, half_cols(0)], dst[:, t, :])
            else:
                store_hinge(u, 0)
        hinge_on_gpsimd(rounded_out(0, QUARTER), margin[0][:, :, quarters[0]].rearrange("p t c -> p c t"))
        add_place(3, 1)
        nc.scalar.activation(hinge_sb[1][1][:, 1, :], margin[1][:, 3, :], RELU)
        add_place(2, 1)
        nc.scalar.activation(hinge_sb[1][1][:, 0, :], margin[1][:, 2, :], RELU)
        store_hinge(1, 1)
        nc.scalar.activation(*out_views(QUARTER, QUARTER), RELU)

        last_margin = [margin[1][:, 0:2, cols] for cols in quarters]
        last_hinge = [hinge_sb[0][1][:, :, cols] for cols in quarters]

        def add_last(c):
            nc.vector.tensor_tensor(last_margin[c], acc_last[c][:], label_third[:, :, quarters[c]], ALU.add)

        vector_round = (HALF - SCALAR_TAIL) // 2
        add_last(0)
        add_last(1)
        for c in range(2):
            nc.vector.tensor_scalar_max(last_hinge[c], last_margin[c], 0.0)
            nc.vector.tensor_scalar_max(*out_views(HALF + c * vector_round, vector_round), 0.0)
        store_hinge(0, 1)
        nc.scalar.activation(*out_views(J - SCALAR_TAIL, SCALAR_TAIL), RELU)
        for c0 in (0, QUARTER):
            quantise_out(c0, QUARTER)
        store_words(0)
        for c0 in (HALF, HALF + QUARTER):
            quantise_out(c0, QUARTER)
        store_words(1)

        for r in range(PACK):
            nc.sync.dma_start(out_scales_i32[r], out_scales[r:P:QUADRANT, :].bitcast(I32))
